import numpy as np, ml_dtypes
CORES = [16,18,20,22]
N = 4
BF = ml_dtypes.bfloat16
def f(rng, *shape):
    return (rng.standard_normal(shape, dtype=np.float32) * np.exp2(rng.integers(-2, 3, shape[:-1] + (1,)))).astype(BF)
def wide(rng, *shape):
    v = f(rng, *shape).astype(np.float32); k = shape[:-2] + (1, shape[-1])
    return (v * np.exp2(rng.integers(-6, 7, k)) * (rng.random(k) > 0.0625)).astype(BF)
def gentries(a):
    return np.ascontiguousarray(a.reshape(8, 16, -1).transpose(0, 2, 1)).reshape(8, -1)
def gtable(e):
    e = np.asarray(e); return np.ascontiguousarray(e.reshape(8, -1, 16).transpose(0, 2, 1)).reshape(128, -1).astype(np.int32)
R, S, P, CAPP, SM = 2048, 32, 32, 640, 512
D, W = 2 * S * P, 512 // P
ST = np.arange(D) // (2 * P)
def draws(a, b, cn):
    u = ((a * np.arange(D) + b) >> 2) & 1023
    m = (u * np.sum(cn, 0)[:, ST]) >> 10
    return m, np.sum(m >= np.add.accumulate(cn, 0)[:, :, ST], 0)
def most(own):
    return np.max(np.stack([np.sum(own == q, 1) for q in range(N)]), 0)
def parts(rng, tot, k, hi):
    v = []
    for i in range(k - 1, -1, -1):
        e = int(rng.integers(max(1, tot - i * hi), min(hi, tot - i) + 1)); v.append(e); tot -= e
    return rng.permutation(v)
def latin(rng, al, small):
    cn = np.zeros((N, 8, S), np.int64); turn = (np.arange(N)[:, None] + np.arange(N)) % N
    for g in range(8):
        t = np.concatenate([[1, SM], parts(rng, R - 1 - SM, S // N - 2, SM)]) if small else parts(rng, R, S // N, SM)
        cn[:, g] = np.concatenate([rng.multinomial(e, rng.dirichlet(np.full(N, al)))[turn] for e in t], 1)[:, rng.permutation(S)]
    return cn
def sole(rng):
    cn = np.zeros((N, 8, S), np.int64); q = rng.integers(0, N); k = CAPP // (2 * P)
    for g in range(8):
        n = [k] + [(S - k + i) // (N - 1) for i in range(N - 1)]; o = rng.permutation(np.repeat((q + g + np.arange(N)) % N, n))
        for i in range(N):
            p = np.flatnonzero(o == i); cn[i, g, p] = parts(rng, R, len(p), SM)
    return cn
def even(rng, ends):
    low = rng.choice([0, W - 1], (8, 1)) if ends else rng.integers(0, W, (8, 1))
    return 4 * W * (2 * rng.integers(0, P, (8, 1)) + 1), 4 * (W * rng.integers(0, 2 * P, (8, 1)) + low) + rng.integers(0, 4, (8, 1))
def keys(rng, cn):
    out = []
    for r in range(N):
        a, b = even(rng, False)
        for t in range(4):
            c, e = rng.integers(256, 3841, (8, 1)), rng.integers(0, 4096, (8, 1)); ok = (most(draws(c, e, cn)[1]) <= CAPP)[:, None]
            a, b = np.where(ok, c, a), np.where(ok, e, b)
        out += [a, b]
    return np.concatenate(out, 1)
def make(rng, cn, ab):
    return {"x": f(rng, N, 128, R), "idx": np.stack([gtable(rng.permuted(np.tile(np.arange(R), (8, 1)), axis=1)) for r in range(N)]),
            "counts": cn.astype(np.int32), "ab": np.tile(ab[None], (N, 1, 1)).astype(np.int32)}
def setup_inputs(rng):
    cn = latin(rng, 2.0, False); return make(rng, cn, keys(rng, cn))
def setup_inputs_full(rng):
    ab = rng.integers(0, 4096, (8, 2 * N)); g = rng.integers(0, 8, N); k = 2 * np.arange(N)
    ab[g, k] = 0; ab[(g + 1) % 8, k] = rng.integers(1, 16, N); ab[(g + 2) % 8, k] = 4095; ab[(g + 3) % 8, k] = rng.integers(1024, 3072, N)
    return make(rng, sole(rng), ab)
def setup_inputs_ends(rng):
    d = make(rng, latin(rng, 1.0, False), np.concatenate([e for r in range(N) for e in even(rng, True)], 1))
    d["idx"] = np.stack([gtable(np.where(rng.random((8, 1)) < 0.5, np.arange(R), np.arange(R)[::-1])) for r in range(N)]); return d
def setup_inputs_uneven(rng):
    cn = latin(rng, 0.2, True); return make(rng, cn, keys(rng, cn))
def setup_inputs_spread(rng):
    d = setup_inputs(rng); d["x"] = wide(rng, N, 128, R); return d
def check_inputs(d):
    bad = []; cn = d["counts"].astype(np.int64); ab = d["ab"].astype(np.int64); sz = np.sum(cn, 0)
    if not np.isfinite(d["x"].astype(np.float32)).all(): bad.append("finite")
    if not all((np.sort(gentries(i), 1) == np.arange(R)).all() for i in d["idx"]): bad.append("each_row_once")
    if cn.min() < 0 or (np.sum(cn, 2) != R).any(): bad.append("counts")
    if sz.min() < 1 or sz.max() > SM: bad.append("sizes")
    if ab.min() < 0 or ab.max() > 4095 or (ab != ab[:1]).any(): bad.append("constants")
    if not bad and any(most(draws(ab[0][:, 2 * r:2 * r + 1], ab[0][:, 2 * r + 1:2 * r + 2], cn)[1]).max() > CAPP for r in range(N)): bad.append("cap")
    return bad
def reference(x, idx, counts, ab):
    cn = counts.astype(np.int64); start = np.add.accumulate(cn, 2) - cn; before = np.add.accumulate(cn, 0) - cn
    rows = np.stack([gentries(i) for i in idx]).astype(np.int64); X = x.astype(np.float32).reshape(N, 8, 16, R)
    G = np.arange(8)[:, None]; y = np.zeros((N, 128, S), np.float32)
    for r in range(N):
        c = ab[r].astype(np.int64); m, own = draws(c[:, 2 * r:2 * r + 1], c[:, 2 * r + 1:2 * r + 2], cn)
        row = rows[own, G, start[own, G, ST] + m - before[own, G, ST]]
        v = X[own, G, :, row].reshape(8, S, P, 2, 16)
        z = np.abs(v[:, :, :, 0] - v[:, :, :, 1]); h = P
        while h > 1:
            h >>= 1; z = z[:, :, :h] + z[:, :, h:]
        y[r] = z[:, :, 0].transpose(0, 2, 1).reshape(128, S)
    return {"y": y}

@@ -1,0 +1,363 @@
+from concourse.bass import DstId, RemoteDMATransfer
+from concourse.mybir import AluOpType, ActivationFunctionType
+
+R = 2048
+H = R // 2
+NB = 2
+NA = 1
+OWN_DMA = True
+W0 = H
+XA0 = 9 * H
+
+SCRATCH = {
+    "big": ("sbuf", [128, 11 * H], "bfloat16"),
+    "bufb": ("sbuf", [128, H], "bfloat16"),
+    "idx32": ("sbuf", [128, 128], "int32"),
+    "offb": ("sbuf", [128, 64], "uint16"),
+    "offa": ("sbuf", [128, 64], "uint16"),
+    "call": ("sbuf", [128, 16], "int32"),
+    "ab32": ("sbuf", [128, 8], "int32"),
+    "abf": ("sbuf", [128, 8], "float32"),
+    "nraw": ("sbuf", [128, 128], "int32"),
+    "n32": ("sbuf", [128, 128], "int32"),
+    "kc0": ("sbuf", [128, 4], "int32"),
+    "kc": ("sbuf", [128, 4], "float32"),
+    "v3": ("sbuf", [128, 128], "bfloat16"),
+    "selg": ("sbuf", [128, 128], "float32"),
+    "vv": ("sbuf", [128, 128], "bfloat16"),
+    "mb": ("sbuf", [128, 128], "float16"),
+    "m1": ("sbuf", [128, 128], "float16"),
+    "m2": ("sbuf", [128, 128], "float16"),
+    "m3": ("sbuf", [128, 128], "float16"),
+    "raw": ("sbuf", [128, 128], "int32"),
+    "u32": ("sbuf", [128, 128], "int32"),
+    "uf": ("sbuf", [128, 128], "float32"),
+    "mem": ("sbuf", [128, 128], "int32"),
+    "t2": ("sbuf", [128, 128], "float32"),
+    "tb": ("sbuf", [128, 128], "float32"),
+    "tc": ("sbuf", [128, 128], "float32"),
+    "off": ("sbuf", [128, 128], "uint16"),
+    "cf2": ("sbuf", [128, 16], "float16"),
+    "vb": ("sbuf", [128, 1024], "bfloat16"),
+    "dd": ("sbuf", [128, 1024], "float32"),
+    "zs": ("sbuf", [128, 512], "float32"),
+    "l1s": ("sbuf", [128, 256], "float32"),
+    "l2": ("sbuf", [128, 256], "float32"),
+    "l3": ("sbuf", [128, 128], "float32"),
+    "l4": ("sbuf", [128, 64], "float32"),
+    "resb": ("sbuf", [128, 32], "float32"),
+    "land": ("sbuf", [128, 32], "float32"),
+    "pab": ("psum", [128, 512], "float32"),
+    "pbef": ("psum", [128, 512], "float32"),
+    "pd": ("psum", [128, 512], "float32"),
+    "pt": ("psum", [128, 512], "float32"),
+    "pz0": ("psum", [128, 512], "float32"),
+    "pz1": ("psum", [128, 512], "float32"),
+    "pl": ("psum", [128, 512], "float32"),
+}
+NLOCAL = 90
+SEMAPHORES = (["cnt", "res", "sent"] + ["p%d_%d" % (q, k) for q in range(4) for k in range(4)]
+              + ["s%d" % i for i in range(NLOCAL)])
+
+ADD, SUB, MUL = AluOpType.add, AluOpType.subtract, AluOpType.mult
+COPY, ABS = ActivationFunctionType.Copy, ActivationFunctionType.Abs
+
+
+def _bits(engines):
+    m = 0
+    for e in engines:
+        m |= 1 << e
+    return m
+
+
+def rank_program(g, core, T, topo):
+    rank = T.rank_of(core)
+    if rank is None:
+        return
+    cores = list(T.cores)
+    n = len(cores)
+    order = sorted(range(n), key=lambda r: (topo.chip(cores[r]), topo.die(cores[r]), r))
+    place = {r: i for i, r in enumerate(order)}
+    t = place[rank] % 2
+    pair = [order[place[rank] - t], order[place[rank] - t + 1]]
+    mate = pair[1 - t]
+    far_same = [r for r in range(n) if r not in pair and place[r] % 2 == t][0]
+    far_other = [r for r in range(n) if r not in pair and place[r] % 2 != t][0]
+    others = [r for r in range(n) if r != rank]
+
+    def dst(r):
+        a = topo.addr(cores[r])
+        return DstId(rid=a[0], pnc=a[1])
+
+    def common(src, rs):
+        return [e for e in topo.engines(cores[src], cores[rs[0]])
+                if all(e in topo.engines(cores[src], cores[r]) for r in rs)]
+
+    V, A, PE, SY = g.vector, g.scalar, g.tensor, g.sync
+    used = [0]
+
+    def tok():
+        used[0] += 1
+        return [T.sem["s%d" % (used[0] - 1)], 0]
+
+    def mark(ins, k=None, by=1):
+        if k is None:
+            k = tok()
+        ins.then_inc(k[0], by)
+        k[1] += by
+        return k
+
+    def wait(q, *ks):
+        for k in ks:
+            q.wait_ge(k[0], k[1])
+
+    lo, hi = slice(0, 64), slice(64, 128)
+    half = (lo, hi)
+    mine, theirs = half[t], half[1 - t]
+    big = T.big
+
+    def lcol(q):
+        return R + R * q
+
+    def zcol(q):
+        return H + R * q
+
+    mycnt = T.call[:, 8 + 2 * rank:10 + 2 * rank]
+    k_cnt = mark(SY.dma_start(mycnt, T.counts[:]), by=16)
+    k_idx = mark(A.dma_start(T.idx32[:], T.idx[:]), by=16)
+    k_ab = mark(SY.dma_start(T.ab32[0:8, :], T.ab[:]), by=16)
+    k_xb = mark(SY.dma_start(big[lo, 0:R], T.x[theirs, :]), by=16)
+    mark(A.dma_start(big[hi, 0:R], T.x[theirs, :]), k_xb, 16)
+    k_xa = mark(SY.dma_start(big[lo, XA0:XA0 + R], T.x[mine, :]), by=16)
+    mark(A.dma_start(big[hi, XA0:XA0 + R], T.x[mine, :]), k_xa, 16)
+
+    k_n = mark(g.iota(T.nraw[:], [[64, 2], [1, 2], [2, 32]], 0, 128))
+    k_v3 = mark(g.iota(T.v3[0:8, :], [[0, 2], [-1, 4], [0, 16]], -4 * t, 1, allow_small_or_imprecise_dtypes=True))
+    k_vv = mark(g.iota(T.vv[:], [[0, 2], [-1, 64]], 0, 1, allow_small_or_imprecise_dtypes=True))
+
+    k_pad = mark(V.memset(T.call[:, 0:8], 0))
+    wait(V, k_n)
+    k_n32 = mark(V.tensor_scalar(T.n32[:], T.nraw[:], 2047, None, AluOpType.bitwise_and))
+    k_kc0 = mark(V.tensor_scalar(T.kc0[:, 0:1], T.nraw[:, 0:1], 3 * R, None, AluOpType.bitwise_and))
+    wait(V, k_v3)
+    k_selg = mark(V.tensor_scalar(T.selg[0:8, :], T.v3[0:8, :], 0.0, None, AluOpType.is_equal))
+    wait(V, k_kc0)
+    k_kc = mark(V.tensor_scalar(T.kc[lo, 0:1], T.kc0[lo, 0:1], -1.0, float(H), MUL, ADD))
+    mark(V.tensor_scalar(T.kc[hi, 0:1], T.kc0[hi, 0:1], -1.0, None, MUL), k_kc)
+    wait(V, k_vv)
+    k_m = tok()
+    for buf, op_lo, op_hi in ((T.m1, AluOpType.is_lt, AluOpType.is_gt), (T.m2, AluOpType.is_lt, AluOpType.is_ge),
+                              (T.m3, AluOpType.is_le, AluOpType.is_gt)):
+        mark(V.tensor_scalar(buf[lo, :], T.vv[lo, :], 0.0, None, op_lo), k_m)
+        mark(V.tensor_scalar(buf[hi, :], T.vv[hi, :], 64.0, -0.75, op_hi, ADD), k_m)
+    mark(V.tensor_scalar(T.mb[lo, :], T.vv[lo, :], 0.0, None, AluOpType.is_equal), k_m)
+    mark(V.tensor_scalar(T.mb[hi, :], T.vv[hi, :], 64.0, None, AluOpType.is_equal), k_m)
+
+    sent = [T.sem.sent, 0]
+    wait(g, k_cnt)
+    e = common(rank, others)
+    g.remote_dma_fused([RemoteDMATransfer(dst_ids=[dst(r) for r in others], dma_engine_mask=_bits(e),
+                                          remote_sem=T.sem.cnt, srcs=[mycnt], dsts=[mycnt] * len(others))],
+                       local_sem=T.sem.sent)
+    sent[1] += len(e)
+    k_call = [T.sem.cnt, sum(len(common(s, [r for r in range(n) if r != s])) for s in others)]
+
+    wait(V, k_ab)
+    k_abf = mark(V.tensor_copy(T.abf[0:8, :], T.ab32[0:8, :]))
+    wait(PE, k_selg, k_abf)
+    k_pab = mark(PE.matmul(T.pab[:, 0:8], T.selg[0:8, :], T.abf[0:8, :], True, True))
+    wait(V, k_idx)
+    k_ob = mark(V.tensor_copy(T.offb[lo, :], T.idx32[theirs, 0:64]))
+    mark(V.tensor_copy(T.offb[hi, :], T.idx32[theirs, 64:128]), k_ob)
+    k_oa = mark(V.tensor_copy(T.offa[lo, :], T.idx32[mine, 0:64]))
+    mark(V.tensor_copy(T.offa[hi, :], T.idx32[mine, 64:128]), k_oa)
+    wait(V, k_pab, k_n32)
+    k_raw = tok()
+    for i in range(2):
+        c = 2 * pair[i]
+        mark(V.tensor_scalar(T.raw[half[i], :], T.n32[half[i], :], T.pab[half[i], c:c + 1],
+                             T.pab[half[i], c + 1:c + 2], MUL, ADD), k_raw)
+    wait(V, k_raw)
+    k_u = mark(V.tensor_scalar(T.u32[:], T.raw[:], 2, 1023, AluOpType.arith_shift_right, AluOpType.bitwise_and))
+    wait(V, k_u)
+    k_uf = mark(V.tensor_scalar(T.uf[:], T.u32[:], 1.0 / 1024, None, MUL))
+
+    def sort(win, offs, out, o0, chunks):
+        ks = []
+        w = H // chunks
+        for k in range(chunks):
+            a, m, b = k * w, k * w + w // 2, (k + 1) * w
+            kk = mark(V.tensor_copy(out[:, o0 + a:o0 + m], win.indirect(offs[:, a // 16:m // 16])))
+            mark(A.activation(out[:, o0 + m:o0 + b], win.indirect(offs[:, m // 16:b // 16]), COPY), kk)
+            ks.append(kk)
+        return ks
+
+    wait(V, k_xb, k_ob)
+    wait(A, k_xb, k_ob)
+    k_sb = sort(big[:, 0:R], T.offb, T.bufb, 0, NB)
+    wait(V, k_xa, k_oa)
+    wait(A, k_xa, k_oa)
+    k_sa = sort(big[:, XA0:XA0 + R], T.offa, big, lcol(rank), NA)
+
+    eb = common(rank, [mate, far_other])
+    wb, wa = H // NB, H // NA
+    for k in range(NB):
+        wait(g, k_sb[k])
+        src = T.bufb[:, k * wb:(k + 1) * wb]
+        to = big[:, lcol(rank) + k * wb:lcol(rank) + (k + 1) * wb]
+        sem = T.sem["p%d_%d" % (rank, k)]
+        g.remote_dma_fused([
+            RemoteDMATransfer(dst_ids=[dst(far_other)], dma_engine_mask=_bits(eb[0::2]), remote_sem=sem, src=src, dst=to),
+            RemoteDMATransfer(dst_ids=[dst(mate)], dma_engine_mask=_bits(eb[1::2]), remote_sem=sem, src=src, dst=to),
+        ], local_sem=T.sem.sent)
+        sent[1] += len(eb)
+    ea = common(rank, [far_same])
+    for k in range(NA):
+        wait(g, k_sa[k])
+        ap = big[:, lcol(rank) + k * wa:lcol(rank) + (k + 1) * wa]
+        a = topo.addr(cores[far_same])
+        g.remote_dma(ap, ap, T.sem["p%d_%d" % (rank, k)], T.sem.sent, a[1], a[0], _bits(ea))
+        sent[1] += len(ea)
+
+    def piece(s, k):
+        if s == far_same:
+            return [T.sem["p%d_%d" % (s, k)], len(common(s, [rank]))]
+        ss = common(s, [rank, far_same])
+        return [T.sem["p%d_%d" % (s, k)], len(ss[1::2] if s == mate else ss[0::2])]
+
+    k_w = tok()
+
+    def cross(q, s, up, a, b):
+        if up:
+            o, i = big[hi, zcol(s) + a:zcol(s) + b], big[lo, lcol(s) + a:lcol(s) + b]
+        else:
+            o, i = big[lo, zcol(s + 1) + a:zcol(s + 1) + b], big[hi, lcol(s) + a:lcol(s) + b]
+        if q == "v":
+            mark(V.tensor_copy(o, i), k_w)
+        elif q == "a":
+            mark(A.activation(o, i, COPY), k_w)
+        else:
+            return SY.dma_start(o, i)
+
+    wait(V, *(k_sb + k_sa))
+    wait(A, *(k_sb + k_sa))
+    full = [k_w]
+    if OWN_DMA:
+        wait(SY, *(k_sb + k_sa))
+        k_own = mark(cross("s", rank, True, 0, H), by=16)
+        mark(cross("s", rank, False, 0, H), k_own, 16)
+        full.append(k_own)
+    else:
+        cross("a", rank, True, 0, H)
+        cross("v", rank, False, 0, H)
+
+    wait(V, k_call, k_cnt, k_pad)
+    k_cf = mark(V.tensor_copy(T.cf2[lo, 0:12], T.call[mine, 4:16]))
+    mark(V.tensor_copy(T.cf2[hi, 0:12], T.call[mine, 2:14]), k_cf)
+    wait(PE, k_m, k_cf)
+    PE.matmul(T.pbef[:, 0:8], T.mb[:], T.cf2[:, 4:12], True, False)
+    k_bef = mark(PE.matmul(T.pbef[:, 0:8], T.mb[:], T.cf2[:, 0:8], False, True))
+    PE.matmul(T.pd[:, 0:4], T.m1[:], T.cf2[:, 4:12:2], True, False)
+    k_d = mark(PE.matmul(T.pd[:, 0:4], T.m2[:], T.cf2[:, 5:12:2], False, True))
+    PE.matmul(T.pd[:, 4:8], T.m3[:], T.cf2[:, 4:12:2], True, False)
+    mark(PE.matmul(T.pd[:, 4:8], T.m1[:], T.cf2[:, 5:12:2], False, True), k_d)
+    wait(V, k_bef, k_uf)
+    k_mem = tok()
+    for sh in range(2):
+        cs = slice(64 * sh, 64 * sh + 64)
+        mark(V.tensor_scalar(T.mem[:, cs], T.uf[:, cs], T.pbef[:, 6 + sh:7 + sh], -0.5 + 1.0 / 2048, MUL, ADD), k_mem)
+    wait(V, k_mem, k_d)
+    k_t = tok()
+    for q in (1, 2, 3):
+        for sh in range(2):
+            c0 = 64 * sh
+            out = T.t2[:, c0:c0 + 64] if q == 2 else T.pt[:, 64 * (q - 1) + c0:64 * (q - 1) + c0 + 64]
+            b = 2 * (q - 1) + sh
+            mark(V.tensor_scalar(out, T.mem[:, c0:c0 + 64], T.pbef[:, b:b + 1], T.pd[:, 4 * sh + q:4 * sh + q + 1],
+                                 AluOpType.is_ge, MUL), k_t)
+    wait(V, k_t)
+    k_s = mark(V.tensor_tensor(T.pt[:, 0:128], T.pt[:, 0:128], T.t2[:], ADD))
+    mark(V.tensor_tensor(T.tb[:], T.pt[:, 128:256], T.mem[:], ADD), k_s)
+    wait(V, k_s)
+    k_c = mark(V.tensor_tensor(T.tc[:], T.pt[:, 0:128], T.tb[:], ADD))
+    wait(V, k_c, k_kc)
+    k_off = tok()
+    for sh in range(2):
+        mark(V.tensor_scalar(T.off[:, sh:128:2], T.tc[:, 64 * sh:64 * sh + 64], T.pd[:, 4 * sh:4 * sh + 1],
+                             T.kc[:, 0:1], ADD, ADD), k_off)
+
+    for k in range(NB):
+        a, b = k * wb, (k + 1) * wb
+        wait(A, piece(mate, k))
+        cross("a", mate, True, a, b)
+        wait(V, piece(far_other, k))
+        cross("v", far_other, True, a, b)
+        cross("v", far_other, False, a, b)
+        if k == 0 and NB > 1:
+            cross("a", mate, False, a, b)
+        else:
+            wait(V, piece(mate, k))
+            cross("v", mate, False, a, b)
+    for k in range(NA):
+        a, b = k * wa, (k + 1) * wa
+        m = a + (wa // 3) // 16 * 16
+        wait(V, piece(far_same, k))
+        wait(A, piece(far_same, k))
+        cross("v", far_same, True, a, b)
+        cross("v", far_same, False, a, m)
+        cross("a", far_same, False, m, b)
+
+    win = big[:, W0:W0 + 9 * H]
+    arrived = [piece(s, k) for s in (mate, far_other) for k in range(NB)] + [piece(far_same, k) for k in range(NA)]
+    wait(V, *(full + arrived + [k_off]))
+    wait(A, *(full + arrived + [k_off]))
+
+    def draw(second, b4, b3):
+        c = 64 * second + 32 * b4 + 16 * b3
+        return win.indirect(T.off[:, c:c + 16])
+
+    def blk(buf, b4, b3):
+        c = 256 * (2 * b4 + b3)
+        return buf[:, c:c + 256]
+
+    seq = [(0, 0), (1, 0), (0, 1), (1, 1)]
+    k_v = {}
+    for b in seq[:3]:
+        k_v[b] = mark(A.activation(blk(T.vb, *b), draw(0, *b), COPY))
+    k_v[seq[3]] = mark(V.tensor_copy(blk(T.vb, *seq[3]), draw(0, *seq[3])))
+    k_z = {0: tok(), 1: tok()}
+    pz = (T.pz0, T.pz1)
+    for b in seq:
+        wait(V, k_v[b])
+        k = mark(V.tensor_tensor(blk(T.dd, *b), draw(1, *b), blk(T.vb, *b), SUB))
+        wait(A, k)
+        out = pz[b[1]][:, 0:256] if b[0] == 0 else T.zs[:, 256 * b[1]:256 * b[1] + 256]
+        mark(A.activation(out, blk(T.dd, *b), ABS), k_z[b[1]])
+    wait(V, k_z[0])
+    k = mark(V.tensor_tensor(T.pl[:, 0:256], T.pz0[:, 0:256], T.zs[:, 0:256], ADD))
+    wait(V, k_z[1])
+    mark(V.tensor_tensor(T.l1s[:], T.pz1[:, 0:256], T.zs[:, 256:512], ADD), k)
+    wait(V, k)
+    k = mark(V.tensor_tensor(T.l2[:], T.pl[:, 0:256], T.l1s[:], ADD))
+    wait(V, k)
+    k = mark(V.tensor_tensor(T.l3[:], T.l2[:, 0:128], T.l2[:, 128:256], ADD))
+    wait(V, k)
+    k = mark(V.tensor_tensor(T.l4[:], T.l3[:, 0:64], T.l3[:, 64:128], ADD))
+    wait(V, k)
+    k_res = tok()
+    for sh in range(2):
+        mark(V.tensor_tensor(T.resb[:, sh:32:2], T.l4[:, 16 * sh:16 * sh + 16], T.l4[:, 32 + 16 * sh:48 + 16 * sh], ADD),
+             k_res)
+
+    wait(g, k_res)
+    a = topo.addr(cores[mate])
+    er = common(rank, [mate])
+    g.remote_dma(T.land[:], T.resb[:], T.sem.res, T.sem.sent, a[1], a[0], _bits(er))
+    sent[1] += len(er)
+    wait(A, k_res)
+    k_y0 = mark(A.dma_start(T.y[mine, :], T.resb[mine, :]), by=16)
+    wait(SY, [T.sem.res, len(common(mate, [rank]))])
+    k_y1 = mark(SY.dma_start(T.y[theirs, :], T.land[mine, :]), by=16)
+    wait(A, k_y0)
+    wait(SY, k_y1)
+    wait(g, sent)

@@ -3,61 +3,35 @@ from concourse.mybir import AluOpType, ActivationFunctionType
 
 R = 2048
 H = R // 2
-NB = 2
-NA = 1
-OWN_DMA = True
+CH_B = [(0, 256, 512), (512, 640, 1024)]
+CH_A = [(0, 256, 512), (512, 768, 1024)]
 W0 = H
 XA0 = 9 * H
 
+F32, BF, I32, U16, F16 = "float32", "bfloat16", "int32", "uint16", "float16"
 SCRATCH = {
-    "big": ("sbuf", [128, 11 * H], "bfloat16"),
-    "bufb": ("sbuf", [128, H], "bfloat16"),
-    "idx32": ("sbuf", [128, 128], "int32"),
-    "offb": ("sbuf", [128, 64], "uint16"),
-    "offa": ("sbuf", [128, 64], "uint16"),
-    "call": ("sbuf", [128, 16], "int32"),
-    "ab32": ("sbuf", [128, 8], "int32"),
-    "abf": ("sbuf", [128, 8], "float32"),
-    "nraw": ("sbuf", [128, 128], "int32"),
-    "n32": ("sbuf", [128, 128], "int32"),
-    "kc0": ("sbuf", [128, 4], "int32"),
-    "kc": ("sbuf", [128, 4], "float32"),
-    "v3": ("sbuf", [128, 128], "bfloat16"),
-    "selg": ("sbuf", [128, 128], "float32"),
-    "vv": ("sbuf", [128, 128], "bfloat16"),
-    "mb": ("sbuf", [128, 128], "float16"),
-    "m1": ("sbuf", [128, 128], "float16"),
-    "m2": ("sbuf", [128, 128], "float16"),
-    "m3": ("sbuf", [128, 128], "float16"),
-    "raw": ("sbuf", [128, 128], "int32"),
-    "u32": ("sbuf", [128, 128], "int32"),
-    "uf": ("sbuf", [128, 128], "float32"),
-    "mem": ("sbuf", [128, 128], "int32"),
-    "t2": ("sbuf", [128, 128], "float32"),
-    "tb": ("sbuf", [128, 128], "float32"),
-    "tc": ("sbuf", [128, 128], "float32"),
-    "off": ("sbuf", [128, 128], "uint16"),
-    "cf2": ("sbuf", [128, 16], "float16"),
-    "vb": ("sbuf", [128, 1024], "bfloat16"),
-    "dd": ("sbuf", [128, 1024], "float32"),
-    "zs": ("sbuf", [128, 512], "float32"),
-    "l1s": ("sbuf", [128, 256], "float32"),
-    "l2": ("sbuf", [128, 256], "float32"),
-    "l3": ("sbuf", [128, 128], "float32"),
-    "l4": ("sbuf", [128, 64], "float32"),
-    "resb": ("sbuf", [128, 32], "float32"),
-    "land": ("sbuf", [128, 32], "float32"),
-    "pab": ("psum", [128, 512], "float32"),
-    "pbef": ("psum", [128, 512], "float32"),
-    "pd": ("psum", [128, 512], "float32"),
-    "pt": ("psum", [128, 512], "float32"),
-    "pz0": ("psum", [128, 512], "float32"),
-    "pz1": ("psum", [128, 512], "float32"),
-    "pl": ("psum", [128, 512], "float32"),
+    "big": ("sbuf", [128, 11 * H], BF), "bufb": ("sbuf", [128, H], BF),
+    "idx32": ("sbuf", [128, 128], I32), "offb": ("sbuf", [128, 64], U16), "offa": ("sbuf", [128, 64], U16),
+    "call": ("sbuf", [128, 16], I32), "ab32": ("sbuf", [128, 8], I32), "abf": ("sbuf", [128, 8], F32),
+    "nraw": ("sbuf", [128, 64], I32), "n32": ("sbuf", [128, 64], I32),
+    "kc0": ("sbuf", [128, 4], I32), "kc": ("sbuf", [128, 4], F32),
+    "v3": ("sbuf", [128, 128], BF), "selg": ("sbuf", [128, 128], F32), "vv": ("sbuf", [128, 128], BF),
+    "ma": ("sbuf", [128, 128], F16), "mc": ("sbuf", [128, 128], F16),
+    "s0": ("sbuf", [128, 128], F16), "s1": ("sbuf", [128, 128], F16),
+    "raw": ("sbuf", [128, 128], I32), "u32": ("sbuf", [128, 128], I32), "uf": ("sbuf", [128, 128], F32),
+    "mem": ("sbuf", [128, 128], I32), "t2": ("sbuf", [128, 128], F32), "tb": ("sbuf", [128, 128], F32),
+    "tc": ("sbuf", [128, 128], F32), "off": ("sbuf", [128, 128], U16), "cf2": ("sbuf", [128, 16], F16),
+    "vb": ("sbuf", [128, 1024], BF), "dd": ("sbuf", [128, 1024], F32), "zs": ("sbuf", [128, 512], F32),
+    "l1": ("sbuf", [128, 256], F32), "l2": ("sbuf", [128, 256], F32), "l3": ("sbuf", [128, 128], F32),
+    "l4": ("sbuf", [128, 64], F32), "resm": ("sbuf", [128, 32], F32), "reso": ("sbuf", [128, 32], F32),
+    "land": ("sbuf", [128, 32], F32),
+    "pab": ("psum", [128, 512], F32), "pbef": ("psum", [128, 512], F32), "pd": ("psum", [128, 512], F32),
+    "pt": ("psum", [128, 512], F32), "pz0": ("psum", [128, 512], F32), "pz1": ("psum", [128, 512], F32),
+    "pl": ("psum", [128, 512], F32),
 }
 NLOCAL = 90
 SEMAPHORES = (["cnt", "res", "sent"] + ["p%d_%d" % (q, k) for q in range(4) for k in range(4)]
-              + ["s%d" % i for i in range(NLOCAL)])
+              + ["k%d" % i for i in range(NLOCAL)])
 
 ADD, SUB, MUL = AluOpType.add, AluOpType.subtract, AluOpType.mult
 COPY, ABS = ActivationFunctionType.Copy, ActivationFunctionType.Abs
@@ -98,7 +72,7 @@ def rank_program(g, core, T, topo):
 
     def tok():
         used[0] += 1
-        return [T.sem["s%d" % (used[0] - 1)], 0]
+        return [T.sem["k%d" % (used[0] - 1)], 0]
 
     def mark(ins, k=None, by=1):
         if k is None:
@@ -125,33 +99,35 @@ def rank_program(g, core, T, topo):
     mycnt = T.call[:, 8 + 2 * rank:10 + 2 * rank]
     k_cnt = mark(SY.dma_start(mycnt, T.counts[:]), by=16)
     k_idx = mark(A.dma_start(T.idx32[:], T.idx[:]), by=16)
-    k_ab = mark(SY.dma_start(T.ab32[0:8, :], T.ab[:]), by=16)
     k_xb = mark(SY.dma_start(big[lo, 0:R], T.x[theirs, :]), by=16)
     mark(A.dma_start(big[hi, 0:R], T.x[theirs, :]), k_xb, 16)
-    k_xa = mark(SY.dma_start(big[lo, XA0:XA0 + R], T.x[mine, :]), by=16)
-    mark(A.dma_start(big[hi, XA0:XA0 + R], T.x[mine, :]), k_xa, 16)
+    k_ab = mark(SY.dma_start(T.ab32[0:8, :], T.ab[:]), by=16)
+    k_xa = mark(A.dma_start(big[hi, XA0:XA0 + R], T.x[mine, :]), by=16)
+    mark(SY.dma_start(big[lo, XA0:XA0 + R], T.x[mine, :]), k_xa, 16)
 
-    k_n = mark(g.iota(T.nraw[:], [[64, 2], [1, 2], [2, 32]], 0, 128))
+    k_n = mark(g.iota(T.nraw[:], [[1, 2], [2, 32]], 0, 64))
     k_v3 = mark(g.iota(T.v3[0:8, :], [[0, 2], [-1, 4], [0, 16]], -4 * t, 1, allow_small_or_imprecise_dtypes=True))
-    k_vv = mark(g.iota(T.vv[:], [[0, 2], [-1, 64]], 0, 1, allow_small_or_imprecise_dtypes=True))
+    k_vv = mark(g.iota(T.vv[:], [[-16, 2], [-32, 4], [-1, 16]], 0, 2, allow_small_or_imprecise_dtypes=True))
 
     k_pad = mark(V.memset(T.call[:, 0:8], 0))
+    k_fill = mark(V.memset(T.resm[hi, :], 0.0))
     wait(V, k_n)
-    k_n32 = mark(V.tensor_scalar(T.n32[:], T.nraw[:], 2047, None, AluOpType.bitwise_and))
-    k_kc0 = mark(V.tensor_scalar(T.kc0[:, 0:1], T.nraw[:, 0:1], 3 * R, None, AluOpType.bitwise_and))
+    k_n0 = mark(V.tensor_scalar(T.n32[:], T.nraw[:], H - 1, None, AluOpType.bitwise_and))
+    k_kc0 = mark(V.tensor_scalar(T.kc0[:, 0:1], T.nraw[:, 0:1], 3 * H, None, AluOpType.bitwise_and))
+    wait(V, k_n0, k_kc0)
+    k_n32 = mark(V.tensor_scalar(T.n32[hi, :], T.n32[hi, :], float(H), None, ADD))
+    k_kc = mark(V.tensor_scalar(T.kc[lo, 0:1], T.kc0[lo, 0:1], -2.0, float(H), MUL, ADD))
+    mark(V.tensor_scalar(T.kc[hi, 0:1], T.kc0[hi, 0:1], -2.0, None, MUL), k_kc)
     wait(V, k_v3)
     k_selg = mark(V.tensor_scalar(T.selg[0:8, :], T.v3[0:8, :], 0.0, None, AluOpType.is_equal))
-    wait(V, k_kc0)
-    k_kc = mark(V.tensor_scalar(T.kc[lo, 0:1], T.kc0[lo, 0:1], -1.0, float(H), MUL, ADD))
-    mark(V.tensor_scalar(T.kc[hi, 0:1], T.kc0[hi, 0:1], -1.0, None, MUL), k_kc)
     wait(V, k_vv)
-    k_m = tok()
-    for buf, op_lo, op_hi in ((T.m1, AluOpType.is_lt, AluOpType.is_gt), (T.m2, AluOpType.is_lt, AluOpType.is_ge),
-                              (T.m3, AluOpType.is_le, AluOpType.is_gt)):
-        mark(V.tensor_scalar(buf[lo, :], T.vv[lo, :], 0.0, None, op_lo), k_m)
-        mark(V.tensor_scalar(buf[hi, :], T.vv[hi, :], 64.0, -0.75, op_hi, ADD), k_m)
-    mark(V.tensor_scalar(T.mb[lo, :], T.vv[lo, :], 0.0, None, AluOpType.is_equal), k_m)
-    mark(V.tensor_scalar(T.mb[hi, :], T.vv[hi, :], 64.0, None, AluOpType.is_equal), k_m)
+    k_m = mark(V.tensor_scalar(T.ma[lo, :], T.vv[lo, :], 0.0, None, AluOpType.is_lt))
+    mark(V.tensor_scalar(T.ma[hi, :], T.vv[hi, :], 128.0, -0.75, AluOpType.is_gt, ADD), k_m)
+    mark(V.tensor_scalar(T.mc[lo, :], T.vv[lo, :], -1.0, None, AluOpType.is_lt), k_m)
+    mark(V.tensor_scalar(T.mc[hi, :], T.vv[hi, :], 128.0, -0.75, AluOpType.is_ge, ADD), k_m)
+    for buf, c in ((T.s0, 0.0), (T.s1, -1.0)):
+        mark(V.tensor_scalar(buf[lo, :], T.vv[lo, :], c, None, AluOpType.is_equal), k_m)
+        mark(V.tensor_scalar(buf[hi, :], T.vv[hi, :], c + 128.0, None, AluOpType.is_equal), k_m)
 
     sent = [T.sem.sent, 0]
     wait(g, k_cnt)
@@ -162,49 +138,55 @@ def rank_program(g, core, T, topo):
     sent[1] += len(e)
     k_call = [T.sem.cnt, sum(len(common(s, [r for r in range(n) if r != s])) for s in others)]
 
-    wait(V, k_ab)
-    k_abf = mark(V.tensor_copy(T.abf[0:8, :], T.ab32[0:8, :]))
-    wait(PE, k_selg, k_abf)
-    k_pab = mark(PE.matmul(T.pab[:, 0:8], T.selg[0:8, :], T.abf[0:8, :], True, True))
     wait(V, k_idx)
     k_ob = mark(V.tensor_copy(T.offb[lo, :], T.idx32[theirs, 0:64]))
     mark(V.tensor_copy(T.offb[hi, :], T.idx32[theirs, 64:128]), k_ob)
     k_oa = mark(V.tensor_copy(T.offa[lo, :], T.idx32[mine, 0:64]))
     mark(V.tensor_copy(T.offa[hi, :], T.idx32[mine, 64:128]), k_oa)
+
+    def sort_v(win, offs, out, o0, ch, k):
+        mark(V.tensor_copy(out[:, o0 + ch[0]:o0 + ch[1]], win.indirect(offs[:, ch[0] // 16:ch[1] // 16])), k)
+
+    def sort_a(win, offs, out, o0, ch, k):
+        mark(A.activation(out[:, o0 + ch[1]:o0 + ch[2]], win.indirect(offs[:, ch[1] // 16:ch[2] // 16]), COPY), k)
+
+    sb = (big[:, 0:R], T.offb, T.bufb, 0)
+    sa = (big[:, XA0:XA0 + R], T.offa, big, lcol(rank))
+    k_sb, k_sa = [tok(), tok()], [tok(), tok()]
+    wait(A, k_xb, k_ob)
+    sort_a(*sb, CH_B[0], k_sb[0])
+    sort_a(*sb, CH_B[1], k_sb[1])
+    wait(A, k_xa, k_oa)
+    sort_a(*sa, CH_A[0], k_sa[0])
+    sort_a(*sa, CH_A[1], k_sa[1])
+
+    wait(V, k_xb, k_ob, k_ab)
+    k_abf = mark(V.tensor_copy(T.abf[0:8, :], T.ab32[0:8, :]))
+    wait(PE, k_selg, k_abf)
+    k_pab = mark(PE.matmul(T.pab[:, 0:8], T.selg[0:8, :], T.abf[0:8, :], True, True))
+    sort_v(*sb, CH_B[0], k_sb[0])
     wait(V, k_pab, k_n32)
     k_raw = tok()
-    for i in range(2):
-        c = 2 * pair[i]
-        mark(V.tensor_scalar(T.raw[half[i], :], T.n32[half[i], :], T.pab[half[i], c:c + 1],
-                             T.pab[half[i], c + 1:c + 2], MUL, ADD), k_raw)
+    for i, r in enumerate((mate, rank)):
+        mark(V.tensor_scalar(T.raw[:, 64 * i:64 * i + 64], T.n32[:], T.pab[:, 2 * r:2 * r + 1],
+                             T.pab[:, 2 * r + 1:2 * r + 2], MUL, ADD), k_raw)
+    sort_v(*sb, CH_B[1], k_sb[1])
     wait(V, k_raw)
     k_u = mark(V.tensor_scalar(T.u32[:], T.raw[:], 2, 1023, AluOpType.arith_shift_right, AluOpType.bitwise_and))
+    wait(V, k_xa, k_oa)
+    sort_v(*sa, CH_A[0], k_sa[0])
     wait(V, k_u)
     k_uf = mark(V.tensor_scalar(T.uf[:], T.u32[:], 1.0 / 1024, None, MUL))
-
-    def sort(win, offs, out, o0, chunks):
-        ks = []
-        w = H // chunks
-        for k in range(chunks):
-            a, m, b = k * w, k * w + w // 2, (k + 1) * w
-            kk = mark(V.tensor_copy(out[:, o0 + a:o0 + m], win.indirect(offs[:, a // 16:m // 16])))
-            mark(A.activation(out[:, o0 + m:o0 + b], win.indirect(offs[:, m // 16:b // 16]), COPY), kk)
-            ks.append(kk)
-        return ks
-
-    wait(V, k_xb, k_ob)
-    wait(A, k_xb, k_ob)
-    k_sb = sort(big[:, 0:R], T.offb, T.bufb, 0, NB)
-    wait(V, k_xa, k_oa)
-    wait(A, k_xa, k_oa)
-    k_sa = sort(big[:, XA0:XA0 + R], T.offa, big, lcol(rank), NA)
+    wait(V, k_call, k_cnt, k_pad)
+    k_cf = mark(V.tensor_copy(T.cf2[lo, 0:12], T.call[mine, 4:16]))
+    mark(V.tensor_copy(T.cf2[hi, 0:12], T.call[mine, 2:14]), k_cf)
+    sort_v(*sa, CH_A[1], k_sa[1])
 
     eb = common(rank, [mate, far_other])
-    wb, wa = H // NB, H // NA
-    for k in range(NB):
+    for k, (a, _, b) in enumerate(CH_B):
         wait(g, k_sb[k])
-        src = T.bufb[:, k * wb:(k + 1) * wb]
-        to = big[:, lcol(rank) + k * wb:lcol(rank) + (k + 1) * wb]
+        src = T.bufb[:, a:b]
+        to = big[:, lcol(rank) + a:lcol(rank) + b]
         sem = T.sem["p%d_%d" % (rank, k)]
         g.remote_dma_fused([
             RemoteDMATransfer(dst_ids=[dst(far_other)], dma_engine_mask=_bits(eb[0::2]), remote_sem=sem, src=src, dst=to),
@@ -212,12 +194,15 @@ def rank_program(g, core, T, topo):
         ], local_sem=T.sem.sent)
         sent[1] += len(eb)
     ea = common(rank, [far_same])
-    for k in range(NA):
+    for k, (a, _, b) in enumerate(CH_A):
         wait(g, k_sa[k])
-        ap = big[:, lcol(rank) + k * wa:lcol(rank) + (k + 1) * wa]
-        a = topo.addr(cores[far_same])
-        g.remote_dma(ap, ap, T.sem["p%d_%d" % (rank, k)], T.sem.sent, a[1], a[0], _bits(ea))
+        ap = big[:, lcol(rank) + a:lcol(rank) + b]
+        ad = topo.addr(cores[far_same])
+        g.remote_dma(ap, ap, T.sem["p%d_%d" % (rank, k)], T.sem.sent, ad[1], ad[0], _bits(ea))
         sent[1] += len(ea)
+    k_go = tok()
+    g.sem_inc(k_go[0], 1)
+    k_go[1] = 1
 
     def piece(s, k):
         if s == far_same:
@@ -226,6 +211,7 @@ def rank_program(g, core, T, topo):
         return [T.sem["p%d_%d" % (s, k)], len(ss[1::2] if s == mate else ss[0::2])]
 
     k_w = tok()
+    k_dma = tok()
 
     def cross(q, s, up, a, b):
         if up:
@@ -237,127 +223,129 @@ def rank_program(g, core, T, topo):
         elif q == "a":
             mark(A.activation(o, i, COPY), k_w)
         else:
-            return SY.dma_start(o, i)
+            mark(SY.dma_start(o, i), k_dma, 16)
 
-    wait(V, *(k_sb + k_sa))
+    wait(SY, *(k_sb + k_sa + [k_go]))
+    cross("s", rank, True, 0, H)
+    cross("s", rank, False, 0, H)
+    wait(SY, piece(mate, 0), piece(mate, 1))
+    cross("s", mate, True, 0, H)
+    cross("s", mate, False, 0, H)
+    far = [(far_other, k, ch) for k, ch in enumerate(CH_B)] + [(far_same, k, ch) for k, ch in enumerate(CH_A)]
     wait(A, *(k_sb + k_sa))
-    full = [k_w]
-    if OWN_DMA:
-        wait(SY, *(k_sb + k_sa))
-        k_own = mark(cross("s", rank, True, 0, H), by=16)
-        mark(cross("s", rank, False, 0, H), k_own, 16)
-        full.append(k_own)
-    else:
-        cross("a", rank, True, 0, H)
-        cross("v", rank, False, 0, H)
+    for s, k, ch in far:
+        wait(A, piece(s, k))
+        cross("a", s, True, ch[0], ch[2])
 
-    wait(V, k_call, k_cnt, k_pad)
-    k_cf = mark(V.tensor_copy(T.cf2[lo, 0:12], T.call[mine, 4:16]))
-    mark(V.tensor_copy(T.cf2[hi, 0:12], T.call[mine, 2:14]), k_cf)
+    def down(i):
+        s, k, ch = far[i]
+        wait(V, piece(s, k))
+        cross("v", s, False, ch[0], ch[2])
+
     wait(PE, k_m, k_cf)
-    PE.matmul(T.pbef[:, 0:8], T.mb[:], T.cf2[:, 4:12], True, False)
-    k_bef = mark(PE.matmul(T.pbef[:, 0:8], T.mb[:], T.cf2[:, 0:8], False, True))
-    PE.matmul(T.pd[:, 0:4], T.m1[:], T.cf2[:, 4:12:2], True, False)
-    k_d = mark(PE.matmul(T.pd[:, 0:4], T.m2[:], T.cf2[:, 5:12:2], False, True))
-    PE.matmul(T.pd[:, 4:8], T.m3[:], T.cf2[:, 4:12:2], True, False)
-    mark(PE.matmul(T.pd[:, 4:8], T.m1[:], T.cf2[:, 5:12:2], False, True), k_d)
+    PE.matmul(T.pbef[:, 0:4], T.s0[:], T.cf2[:, 4:12:2], True, False)
+    PE.matmul(T.pbef[:, 0:4], T.s0[:], T.cf2[:, 0:8:2], False, False)
+    PE.matmul(T.pbef[:, 0:4], T.s1[:], T.cf2[:, 5:12:2], False, False)
+    k_bef = mark(PE.matmul(T.pbef[:, 0:4], T.s1[:], T.cf2[:, 1:8:2], False, True))
+    PE.matmul(T.pd[:, 0:4], T.ma[:], T.cf2[:, 4:12:2], True, False)
+    k_d = mark(PE.matmul(T.pd[:, 0:4], T.mc[:], T.cf2[:, 5:12:2], False, True))
     wait(V, k_bef, k_uf)
-    k_mem = tok()
-    for sh in range(2):
-        cs = slice(64 * sh, 64 * sh + 64)
-        mark(V.tensor_scalar(T.mem[:, cs], T.uf[:, cs], T.pbef[:, 6 + sh:7 + sh], -0.5 + 1.0 / 2048, MUL, ADD), k_mem)
+    k_mem = mark(V.tensor_scalar(T.mem[:], T.uf[:], T.pbef[:, 3:4], -0.5 + 1.0 / 2048, MUL, ADD))
     wait(V, k_mem, k_d)
     k_t = tok()
-    for q in (1, 2, 3):
-        for sh in range(2):
-            c0 = 64 * sh
-            out = T.t2[:, c0:c0 + 64] if q == 2 else T.pt[:, 64 * (q - 1) + c0:64 * (q - 1) + c0 + 64]
-            b = 2 * (q - 1) + sh
-            mark(V.tensor_scalar(out, T.mem[:, c0:c0 + 64], T.pbef[:, b:b + 1], T.pd[:, 4 * sh + q:4 * sh + q + 1],
-                                 AluOpType.is_ge, MUL), k_t)
+    for q, out in ((1, T.pt[:, 0:128]), (2, T.t2[:]), (3, T.pt[:, 128:256])):
+        mark(V.tensor_scalar(out, T.mem[:], T.pbef[:, q - 1:q], T.pd[:, q:q + 1], AluOpType.is_ge, MUL), k_t)
+    wait(V, *(k_sb + k_sa))
+    down(0)
     wait(V, k_t)
     k_s = mark(V.tensor_tensor(T.pt[:, 0:128], T.pt[:, 0:128], T.t2[:], ADD))
     mark(V.tensor_tensor(T.tb[:], T.pt[:, 128:256], T.mem[:], ADD), k_s)
+    down(1)
     wait(V, k_s)
     k_c = mark(V.tensor_tensor(T.tc[:], T.pt[:, 0:128], T.tb[:], ADD))
-    wait(V, k_c, k_kc)
-    k_off = tok()
-    for sh in range(2):
-        mark(V.tensor_scalar(T.off[:, sh:128:2], T.tc[:, 64 * sh:64 * sh + 64], T.pd[:, 4 * sh:4 * sh + 1],
-                             T.kc[:, 0:1], ADD, ADD), k_off)
-
-    for k in range(NB):
-        a, b = k * wb, (k + 1) * wb
-        wait(A, piece(mate, k))
-        cross("a", mate, True, a, b)
-        wait(V, piece(far_other, k))
-        cross("v", far_other, True, a, b)
-        cross("v", far_other, False, a, b)
-        if k == 0 and NB > 1:
-            cross("a", mate, False, a, b)
-        else:
-            wait(V, piece(mate, k))
-            cross("v", mate, False, a, b)
-    for k in range(NA):
-        a, b = k * wa, (k + 1) * wa
-        m = a + (wa // 3) // 16 * 16
-        wait(V, piece(far_same, k))
-        wait(A, piece(far_same, k))
-        cross("v", far_same, True, a, b)
-        cross("v", far_same, False, a, m)
-        cross("a", far_same, False, m, b)
+    down(2)
+    wait(V, k_c, k_kc, k_fill)
+    k_off = mark(V.tensor_scalar(T.off[:], T.tc[:], T.pd[:, 0:1], T.kc[:, 0:1], ADD, ADD))
+    down(3)
 
     win = big[:, W0:W0 + 9 * H]
-    arrived = [piece(s, k) for s in (mate, far_other) for k in range(NB)] + [piece(far_same, k) for k in range(NA)]
-    wait(V, *(full + arrived + [k_off]))
-    wait(A, *(full + arrived + [k_off]))
+    wait(V, k_off, k_dma, k_w)
+    wait(A, k_off, k_dma, k_w)
 
-    def draw(second, b4, b3):
-        c = 64 * second + 32 * b4 + 16 * b3
+    def draw(who, second, b):
+        c = 64 * who + 32 * second + 16 * b
         return win.indirect(T.off[:, c:c + 16])
 
-    def blk(buf, b4, b3):
-        c = 256 * (2 * b4 + b3)
+    def blk(buf, who, b):
+        c = 512 * who + 256 * b
         return buf[:, c:c + 256]
 
-    seq = [(0, 0), (1, 0), (0, 1), (1, 1)]
-    k_v = {}
-    for b in seq[:3]:
-        k_v[b] = mark(A.activation(blk(T.vb, *b), draw(0, *b), COPY))
-    k_v[seq[3]] = mark(V.tensor_copy(blk(T.vb, *seq[3]), draw(0, *seq[3])))
-    k_z = {0: tok(), 1: tok()}
     pz = (T.pz0, T.pz1)
-    for b in seq:
-        wait(V, k_v[b])
-        k = mark(V.tensor_tensor(blk(T.dd, *b), draw(1, *b), blk(T.vb, *b), SUB))
-        wait(A, k)
-        out = pz[b[1]][:, 0:256] if b[0] == 0 else T.zs[:, 256 * b[1]:256 * b[1] + 256]
-        mark(A.activation(out, blk(T.dd, *b), ABS), k_z[b[1]])
-    wait(V, k_z[0])
-    k = mark(V.tensor_tensor(T.pl[:, 0:256], T.pz0[:, 0:256], T.zs[:, 0:256], ADD))
-    wait(V, k_z[1])
-    mark(V.tensor_tensor(T.l1s[:], T.pz1[:, 0:256], T.zs[:, 256:512], ADD), k)
-    wait(V, k)
-    k = mark(V.tensor_tensor(T.l2[:], T.pl[:, 0:256], T.l1s[:], ADD))
-    wait(V, k)
-    k = mark(V.tensor_tensor(T.l3[:], T.l2[:, 0:128], T.l2[:, 128:256], ADD))
-    wait(V, k)
-    k = mark(V.tensor_tensor(T.l4[:], T.l3[:, 0:64], T.l3[:, 64:128], ADD))
-    wait(V, k)
-    k_res = tok()
-    for sh in range(2):
-        mark(V.tensor_tensor(T.resb[:, sh:32:2], T.l4[:, 16 * sh:16 * sh + 16], T.l4[:, 32 + 16 * sh:48 + 16 * sh], ADD),
-             k_res)
+    k_z = [tok(), tok()]
 
-    wait(g, k_res)
-    a = topo.addr(cores[mate])
+    def first(q, who, b):
+        if q == "a":
+            return mark(A.activation(blk(T.vb, who, b), draw(who, 0, b), COPY))
+        return mark(V.tensor_copy(blk(T.vb, who, b), draw(who, 0, b)))
+
+    def diff(k, who, b):
+        wait(V, k)
+        return mark(V.tensor_tensor(blk(T.dd, who, b), draw(who, 1, b), blk(T.vb, who, b), SUB))
+
+    def size(k, who, b):
+        wait(A, k)
+        out = pz[who][:, 0:256] if b == 0 else T.zs[:, 256 * who:256 * who + 256]
+        mark(A.activation(out, blk(T.dd, who, b), ABS), k_z[who])
+
+    def level(i, who, k):
+        c, d, f = 128 * who, 64 * who, 32 * who
+        wait(V, k)
+        if i == 1:
+            k = mark(V.tensor_tensor(T.pl[:, c:c + 128], pz[who][:, 0:128], T.zs[:, 2 * c:2 * c + 128], ADD))
+            return mark(V.tensor_tensor(T.l1[:, c:c + 128], pz[who][:, 128:256], T.zs[:, 2 * c + 128:2 * c + 256], ADD), k)
+        if i == 2:
+            return mark(V.tensor_tensor(T.l2[:, c:c + 128], T.pl[:, c:c + 128], T.l1[:, c:c + 128], ADD))
+        if i == 3:
+            return mark(V.tensor_tensor(T.l3[:, d:d + 64], T.l2[:, c:c + 64], T.l2[:, c + 64:c + 128], ADD))
+        if i == 4:
+            return mark(V.tensor_tensor(T.l4[:, f:f + 32], T.l3[:, d:d + 32], T.l3[:, d + 32:d + 64], ADD))
+        res = (T.resm, T.reso)[who]
+        k = tok()
+        for h in range(2):
+            mark(V.tensor_tensor(res[lo, 16 * h:16 * h + 16], T.l4[half[h], f:f + 16], T.l4[half[h], f + 16:f + 32], ADD), k)
+        return k
+
+    v00 = first("a", 0, 0)
+    v01 = first("v", 0, 1)
+    v10 = first("a", 1, 0)
+    d00 = diff(v00, 0, 0)
+    size(d00, 0, 0)
+    d01 = diff(v01, 0, 1)
+    size(d01, 0, 1)
+    v11 = first("a", 1, 1)
+    d10 = diff(v10, 1, 0)
+    size(d10, 1, 0)
+    km = level(1, 0, k_z[0])
+    d11 = diff(v11, 1, 1)
+    size(d11, 1, 1)
+    km = level(2, 0, km)
+    km = level(3, 0, km)
+    km = level(4, 0, km)
+    ko = level(1, 1, k_z[1])
+    k_resm = level(5, 0, km)
+    for i in (2, 3, 4, 5):
+        ko = level(i, 1, ko)
+    k_reso = ko
+
+    wait(g, k_resm)
+    ad = topo.addr(cores[mate])
     er = common(rank, [mate])
-    g.remote_dma(T.land[:], T.resb[:], T.sem.res, T.sem.sent, a[1], a[0], _bits(er))
+    g.remote_dma(T.land[:], T.resm[:], T.sem.res, T.sem.sent, ad[1], ad[0], _bits(er))
     sent[1] += len(er)
-    wait(A, k_res)
-    k_y0 = mark(A.dma_start(T.y[mine, :], T.resb[mine, :]), by=16)
+    wait(A, k_reso)
+    k_y0 = mark(A.dma_start(T.y[mine, :], T.reso[lo, :]), by=16)
     wait(SY, [T.sem.res, len(common(mate, [rank]))])
-    k_y1 = mark(SY.dma_start(T.y[theirs, :], T.land[mine, :]), by=16)
+    k_y1 = mark(SY.dma_start(T.y[theirs, :], T.land[lo, :]), by=16)
     wait(A, k_y0)
     wait(SY, k_y1)
     wait(g, sent)

@@ -7,6 +7,18 @@ CH_B = [(0, 256, 512), (512, 640, 1024)]
 CH_A = [(0, 256, 512), (512, 768, 1024)]
 W0 = H
 XA0 = 9 * H
+LOAD_S = "cnt xb0 ab xa0 xa1"
+LOAD_A = "idx xb1"
+IOTA = "vv n v3"
+IOTA2 = ""
+PRE_V = "eq n0 c0 ob c1 oa h0 sB0 h1 sB1 h2 sA0 cf sA1 mem Fd0 cmp Fd1 add Sd0 sum Sd1 off"
+PRE_A = "sg0 sg1 sq sB0 sB1 sA0 sA1 Fu0 Fu1 Su0 Su1"
+PRE_S = "Ou Od Mu Md"
+DRAW_V = "f1 d0 d1 d2 d3 M1 M2 M3 O1 M4 O2 O3 O4 O5"
+DRAW_A = "f0 f2 f3 a0 a1 a2 a3"
+FOLD = True
+MERGED = False
+TWO = ("M4", "O5")
 
 F32, BF, I32, U16, F16 = "float32", "bfloat16", "int32", "uint16", "float16"
 SCRATCH = {
@@ -16,25 +28,28 @@ SCRATCH = {
     "nraw": ("sbuf", [128, 64], I32), "n32": ("sbuf", [128, 64], I32),
     "kc0": ("sbuf", [128, 4], I32), "kc": ("sbuf", [128, 4], F32),
     "v3": ("sbuf", [128, 128], BF), "selg": ("sbuf", [128, 128], F32), "vv": ("sbuf", [128, 128], BF),
-    "ma": ("sbuf", [128, 128], F16), "mc": ("sbuf", [128, 128], F16),
-    "s0": ("sbuf", [128, 128], F16), "s1": ("sbuf", [128, 128], F16),
+    "ma": ("sbuf", [128, 128], BF), "mc": ("sbuf", [128, 128], BF), "mq": ("sbuf", [128, 128], BF),
+    "s0": ("sbuf", [128, 128], BF), "s1": ("sbuf", [128, 128], BF),
     "raw": ("sbuf", [128, 128], I32), "u32": ("sbuf", [128, 128], I32), "uf": ("sbuf", [128, 128], F32),
-    "mem": ("sbuf", [128, 128], I32), "t2": ("sbuf", [128, 128], F32), "tb": ("sbuf", [128, 128], F32),
-    "tc": ("sbuf", [128, 128], F32), "off": ("sbuf", [128, 128], U16), "cf2": ("sbuf", [128, 16], F16),
+    "mem": ("sbuf", [128, 128], F16), "t1": ("sbuf", [128, 128], F32), "t2": ("sbuf", [128, 128], F32),
+    "s0q": ("sbuf", [128, 128], BF), "s1q": ("sbuf", [128, 128], BF),
+    "neg": ("sbuf", [128, 128], BF), "ident": ("sbuf", [128, 128], F32),
+    "pi": ("psum", [128, 512], F32), "po": ("psum", [128, 512], F32),
+    "t3": ("sbuf", [128, 128], F32), "off": ("sbuf", [128, 128], U16), "cf2": ("sbuf", [128, 16], F16),
     "vb": ("sbuf", [128, 1024], BF), "dd": ("sbuf", [128, 1024], F32), "zs": ("sbuf", [128, 512], F32),
     "l1": ("sbuf", [128, 256], F32), "l2": ("sbuf", [128, 256], F32), "l3": ("sbuf", [128, 128], F32),
-    "l4": ("sbuf", [128, 64], F32), "resm": ("sbuf", [128, 32], F32), "reso": ("sbuf", [128, 32], F32),
-    "land": ("sbuf", [128, 32], F32),
+    "l4": ("sbuf", [128, 64], F32), "res": ("sbuf", [128, 32], F32), "land": ("sbuf", [128, 16], F32),
+    "l4m": ("sbuf", [128, 64], F32), "land3": ("sbuf", [128, 3, 16], F32),
     "pab": ("psum", [128, 512], F32), "pbef": ("psum", [128, 512], F32), "pd": ("psum", [128, 512], F32),
     "pt": ("psum", [128, 512], F32), "pz0": ("psum", [128, 512], F32), "pz1": ("psum", [128, 512], F32),
-    "pl": ("psum", [128, 512], F32),
 }
 NLOCAL = 90
-SEMAPHORES = (["cnt", "res", "sent"] + ["p%d_%d" % (q, k) for q in range(4) for k in range(4)]
+SEMAPHORES = (["cnt", "res", "sent"] + ["p%s%d" % (q, k) for q in "MFS" for k in range(4)]
               + ["k%d" % i for i in range(NLOCAL)])
 
 ADD, SUB, MUL = AluOpType.add, AluOpType.subtract, AluOpType.mult
 COPY, ABS = ActivationFunctionType.Copy, ActivationFunctionType.Abs
+SIGN, IDENT = ActivationFunctionType.Sign, ActivationFunctionType.Identity
 
 
 def _bits(engines):
@@ -58,6 +73,8 @@ def rank_program(g, core, T, topo):
     far_same = [r for r in range(n) if r not in pair and place[r] % 2 == t][0]
     far_other = [r for r in range(n) if r not in pair and place[r] % 2 != t][0]
     others = [r for r in range(n) if r != rank]
+    who_is = {"O": rank, "M": mate, "F": far_other, "S": far_same}
+    chunks = {"O": CH_A, "S": CH_A, "M": CH_B, "F": CH_B, "A": CH_A, "B": CH_B}
 
     def dst(r):
         a = topo.addr(cores[r])
@@ -68,11 +85,12 @@ def rank_program(g, core, T, topo):
                 if all(e in topo.engines(cores[src], cores[r]) for r in rs)]
 
     V, A, PE, SY = g.vector, g.scalar, g.tensor, g.sync
+    queues = [V, A, PE, SY, g]
     used = [0]
 
-    def tok():
+    def tok(total=0):
         used[0] += 1
-        return [T.sem["k%d" % (used[0] - 1)], 0]
+        return [T.sem["k%d" % (used[0] - 1)], total, "k%d" % used[0]]
 
     def mark(ins, k=None, by=1):
         if k is None:
@@ -81,271 +99,380 @@ def rank_program(g, core, T, topo):
         k[1] += by
         return k
 
+    named = {}
+
+    def K(name, total=1):
+        if name not in named:
+            named[name] = tok(total)
+        return named[name]
+
+    def fin(ins, k, by=1):
+        ins.then_inc(k[0], by)
+
+    seen = {}
+
     def wait(q, *ks):
         for k in ks:
-            q.wait_ge(k[0], k[1])
+            key = (queues.index(q), k[2])
+            if seen.get(key, 0) < k[1]:
+                seen[key] = k[1]
+                q.wait_ge(k[0], k[1])
 
     lo, hi = slice(0, 64), slice(64, 128)
     half = (lo, hi)
     mine, theirs = half[t], half[1 - t]
     big = T.big
 
-    def lcol(q):
-        return R + R * q
-
-    def zcol(q):
-        return H + R * q
+    def lcol(r):
+        return R + R * r
 
     mycnt = T.call[:, 8 + 2 * rank:10 + 2 * rank]
-    k_cnt = mark(SY.dma_start(mycnt, T.counts[:]), by=16)
-    k_idx = mark(A.dma_start(T.idx32[:], T.idx[:]), by=16)
-    k_xb = mark(SY.dma_start(big[lo, 0:R], T.x[theirs, :]), by=16)
-    mark(A.dma_start(big[hi, 0:R], T.x[theirs, :]), k_xb, 16)
-    k_ab = mark(SY.dma_start(T.ab32[0:8, :], T.ab[:]), by=16)
-    k_xa = mark(A.dma_start(big[hi, XA0:XA0 + R], T.x[mine, :]), by=16)
-    mark(SY.dma_start(big[lo, XA0:XA0 + R], T.x[mine, :]), k_xa, 16)
+    loads = {"cnt": (mycnt, T.counts[:], K("cnt", 16)), "idx": (T.idx32[:], T.idx[:], K("idx", 16)),
+             "ab": (T.ab32[0:8, :], T.ab[:], K("ab", 16))}
+    for h in range(2):
+        loads["xb%d" % h] = (big[half[h], 0:R], T.x[theirs, :], K("xb", 32))
+        loads["xa%d" % h] = (big[half[h], XA0:XA0 + R], T.x[mine, :], K("xa", 32))
+    for q, names in ((SY, LOAD_S), (A, LOAD_A)):
+        for name in names.split():
+            o, i, k = loads[name]
+            fin(q.dma_start(o, i), k, 16)
 
-    k_n = mark(g.iota(T.nraw[:], [[1, 2], [2, 32]], 0, 64))
-    k_v3 = mark(g.iota(T.v3[0:8, :], [[0, 2], [-1, 4], [0, 16]], -4 * t, 1, allow_small_or_imprecise_dtypes=True))
-    k_vv = mark(g.iota(T.vv[:], [[-16, 2], [-32, 4], [-1, 16]], 0, 2, allow_small_or_imprecise_dtypes=True))
+    k_n, k_v3, k_vv = K("n"), K("v3"), [K("vv")] * 2
+    vv_pat = [[-16, 2], [-32, 4], [-1, 16]]
+    def iotas(names):
+        for name in names.split():
+            if name == "n":
+                fin(g.iota(T.nraw[:], [[1, 2], [2, 32]], 0, 64), k_n)
+            elif name == "v3":
+                fin(g.iota(T.v3[0:8, :], [[0, 2], [-1, 4], [0, 16]], -4 * t, 1, allow_small_or_imprecise_dtypes=True),
+                    k_v3)
+            else:
+                fin(g.iota(T.vv[:], vv_pat, 0, 2, allow_small_or_imprecise_dtypes=True), k_vv[0])
+
+    iotas(IOTA)
 
     k_pad = mark(V.memset(T.call[:, 0:8], 0))
-    k_fill = mark(V.memset(T.resm[hi, :], 0.0))
-    wait(V, k_n)
-    k_n0 = mark(V.tensor_scalar(T.n32[:], T.nraw[:], H - 1, None, AluOpType.bitwise_and))
-    k_kc0 = mark(V.tensor_scalar(T.kc0[:, 0:1], T.nraw[:, 0:1], 3 * H, None, AluOpType.bitwise_and))
-    wait(V, k_n0, k_kc0)
-    k_n32 = mark(V.tensor_scalar(T.n32[hi, :], T.n32[hi, :], float(H), None, ADD))
-    k_kc = mark(V.tensor_scalar(T.kc[lo, 0:1], T.kc0[lo, 0:1], -2.0, float(H), MUL, ADD))
-    mark(V.tensor_scalar(T.kc[hi, 0:1], T.kc0[hi, 0:1], -2.0, None, MUL), k_kc)
-    wait(V, k_v3)
-    k_selg = mark(V.tensor_scalar(T.selg[0:8, :], T.v3[0:8, :], 0.0, None, AluOpType.is_equal))
-    wait(V, k_vv)
-    k_m = mark(V.tensor_scalar(T.ma[lo, :], T.vv[lo, :], 0.0, None, AluOpType.is_lt))
-    mark(V.tensor_scalar(T.ma[hi, :], T.vv[hi, :], 128.0, -0.75, AluOpType.is_gt, ADD), k_m)
-    mark(V.tensor_scalar(T.mc[lo, :], T.vv[lo, :], -1.0, None, AluOpType.is_lt), k_m)
-    mark(V.tensor_scalar(T.mc[hi, :], T.vv[hi, :], 128.0, -0.75, AluOpType.is_ge, ADD), k_m)
-    for buf, c in ((T.s0, 0.0), (T.s1, -1.0)):
-        mark(V.tensor_scalar(buf[lo, :], T.vv[lo, :], c, None, AluOpType.is_equal), k_m)
-        mark(V.tensor_scalar(buf[hi, :], T.vv[hi, :], c + 128.0, None, AluOpType.is_equal), k_m)
+    k_fill = mark(V.memset(T.l4m[hi, :], 0.0)) if "M4" in TWO else k_pad
+    k_n0, k_kc0 = K("n0"), K("kc0")
 
-    sent = [T.sem.sent, 0]
-    wait(g, k_cnt)
+    sent = [T.sem.sent, 0, "sent"]
+    wait(g, K("cnt"))
     e = common(rank, others)
     g.remote_dma_fused([RemoteDMATransfer(dst_ids=[dst(r) for r in others], dma_engine_mask=_bits(e),
                                           remote_sem=T.sem.cnt, srcs=[mycnt], dsts=[mycnt] * len(others))],
                        local_sem=T.sem.sent)
     sent[1] += len(e)
-    k_call = [T.sem.cnt, sum(len(common(s, [r for r in range(n) if r != s])) for s in others)]
+    k_call = [T.sem.cnt, sum(len(common(s, [r for r in range(n) if r != s])) for s in others), "cnt"]
+    iotas(IOTA2)
 
-    wait(V, k_idx)
-    k_ob = mark(V.tensor_copy(T.offb[lo, :], T.idx32[theirs, 0:64]))
-    mark(V.tensor_copy(T.offb[hi, :], T.idx32[theirs, 64:128]), k_ob)
-    k_oa = mark(V.tensor_copy(T.offa[lo, :], T.idx32[mine, 0:64]))
-    mark(V.tensor_copy(T.offa[hi, :], T.idx32[mine, 64:128]), k_oa)
+    def sorted_(p, k):
+        a, m, b = chunks[p][k]
+        return K("s%s%d" % (p, k), (m > a) + (b > m))
 
-    def sort_v(win, offs, out, o0, ch, k):
-        mark(V.tensor_copy(out[:, o0 + ch[0]:o0 + ch[1]], win.indirect(offs[:, ch[0] // 16:ch[1] // 16])), k)
+    k_sb = [sorted_("B", k) for k in range(len(CH_B))]
+    k_sa = [sorted_("A", k) for k in range(len(CH_A))]
 
-    def sort_a(win, offs, out, o0, ch, k):
-        mark(A.activation(out[:, o0 + ch[1]:o0 + ch[2]], win.indirect(offs[:, ch[1] // 16:ch[2] // 16]), COPY), k)
+    def piece(p, k):
+        if p == "O":
+            return k_sa[k]
+        name = "p%s%d" % (p, k)
+        if p == "S":
+            return [T.sem[name], len(common(far_same, [rank])), name]
+        ss = common(who_is[p], [rank, far_same])
+        return [T.sem[name], len(ss[1::2] if p == "M" else ss[0::2]), name]
 
-    sb = (big[:, 0:R], T.offb, T.bufb, 0)
-    sa = (big[:, XA0:XA0 + R], T.offa, big, lcol(rank))
-    k_sb, k_sa = [tok(), tok()], [tok(), tok()]
-    wait(A, k_xb, k_ob)
-    sort_a(*sb, CH_B[0], k_sb[0])
-    sort_a(*sb, CH_B[1], k_sb[1])
-    wait(A, k_xa, k_oa)
-    sort_a(*sa, CH_A[0], k_sa[0])
-    sort_a(*sa, CH_A[1], k_sa[1])
+    k_w, k_dma = tok(), tok()
 
-    wait(V, k_xb, k_ob, k_ab)
-    k_abf = mark(V.tensor_copy(T.abf[0:8, :], T.ab32[0:8, :]))
-    wait(PE, k_selg, k_abf)
-    k_pab = mark(PE.matmul(T.pab[:, 0:8], T.selg[0:8, :], T.abf[0:8, :], True, True))
-    sort_v(*sb, CH_B[0], k_sb[0])
-    wait(V, k_pab, k_n32)
-    k_raw = tok()
-    for i, r in enumerate((mate, rank)):
-        mark(V.tensor_scalar(T.raw[:, 64 * i:64 * i + 64], T.n32[:], T.pab[:, 2 * r:2 * r + 1],
-                             T.pab[:, 2 * r + 1:2 * r + 2], MUL, ADD), k_raw)
-    sort_v(*sb, CH_B[1], k_sb[1])
-    wait(V, k_raw)
-    k_u = mark(V.tensor_scalar(T.u32[:], T.raw[:], 2, 1023, AluOpType.arith_shift_right, AluOpType.bitwise_and))
-    wait(V, k_xa, k_oa)
-    sort_v(*sa, CH_A[0], k_sa[0])
-    wait(V, k_u)
-    k_uf = mark(V.tensor_scalar(T.uf[:], T.u32[:], 1.0 / 1024, None, MUL))
-    wait(V, k_call, k_cnt, k_pad)
-    k_cf = mark(V.tensor_copy(T.cf2[lo, 0:12], T.call[mine, 4:16]))
-    mark(V.tensor_copy(T.cf2[hi, 0:12], T.call[mine, 2:14]), k_cf)
-    sort_v(*sa, CH_A[1], k_sa[1])
+    def pre(q, name):
+        if name[0] == "s" and name[1] in "AB":
+            p, k = name[1], int(name[2])
+            a, m, b = chunks[p][k]
+            a, b = (a, m) if q is V else (m, b)
+            win, offs, out, o = ((big[:, 0:R], T.offb, T.bufb, 0) if p == "B"
+                                 else (big[:, XA0:XA0 + R], T.offa, big, lcol(rank)))
+            wait(q, K("x" + p.lower()), K("o" + p.lower(), 2))
+            src = win.indirect(offs[:, a // 16:b // 16])
+            fin(V.tensor_copy(out[:, o + a:o + b], src) if q is V else A.activation(out[:, o + a:o + b], src, COPY),
+                sorted_(p, k))
+        elif name[0] in who_is:
+            p, up = name[0], name[1] == "u"
+            a, b = (512 * int(name[2]), 512 * int(name[2]) + 512) if name[2:] else (0, H)
+            ks = [k for k, ch in enumerate(chunks[p]) if ch[0] < b and a < ch[2]]
+            wait(q, *[piece(p, k) for k in ks])
+            if up and who_is[p] == 0:
+                wait(q, *k_sb)
+            if not up and who_is[p] == n - 1:
+                wait(q, *k_sa)
+            c = lcol(who_is[p])
+            o, i = ((big[hi, c - H + a:c - H + b], big[lo, c + a:c + b]) if up
+                    else (big[lo, c + H + a:c + H + b], big[hi, c + a:c + b]))
+            if q is V:
+                mark(V.tensor_copy(o, i), k_w)
+            elif q is A:
+                mark(A.activation(o, i, COPY), k_w)
+            else:
+                mark(SY.dma_start(o, i), k_dma, 16)
+        elif name == "go":
+            wait(q, K("go"))
+        elif name in ("ob", "oa"):
+            wait(V, K("idx"))
+            buf, part = (T.offb, theirs) if name == "ob" else (T.offa, mine)
+            for h in range(2):
+                fin(V.tensor_copy(buf[half[h], :], T.idx32[part, 64 * h:64 * h + 64]), K(name, 2))
+        elif name == "sg0":
+            wait(A, k_vv[0])
+            fin(A.activation(T.ma[lo, :], T.vv[lo, :], SIGN, bias=-0.5, scale=-1.0), K("m", 5))
+            fin(A.activation(T.mc[lo, :], T.vv[lo, :], SIGN, bias=-1.5, scale=-1.0), K("m", 5))
+        elif name == "sg1":
+            wait(A, k_vv[1])
+            fin(A.activation(T.ma[hi, :], T.vv[hi, :], SIGN, bias=-128.5), K("m", 5))
+            fin(A.activation(T.mc[hi, :], T.vv[hi, :], SIGN, bias=-127.5), K("m", 5))
+            fin(A.activation(T.mq[:], T.vv[:], IDENT, bias=0.25, scale=0.0), K("m", 5))
+        elif name == "eq":
+            wait(V, *k_vv)
+            for buf, c in ((T.s0, 0.0), (T.s1, -1.0)):
+                for h in range(2):
+                    fin(V.tensor_scalar(buf[half[h], :], T.vv[half[h], :], c + 128.0 * h, -2.0, AluOpType.is_equal,
+                                        MUL), K("eq", 4))
+            if "ide" in PRE_A:
+                wait(PE, K("eq", 4))
+                PE.matmul(T.pi[:, 0:128], T.s0[lo, :], T.s0[lo, :], True, False)
+                fin(PE.matmul(T.pi[:, 0:128], T.s1[lo, :], T.s1[lo, :], False, True), K("pi"))
+        elif name == "sq":
+            wait(A, K("eq", 4))
+            fin(A.activation(T.s0q[:], T.s0[:], COPY, scale=1.0 / 1024), K("sq", 2))
+            fin(A.activation(T.s1q[:], T.s1[:], COPY, scale=1.0 / 1024), K("sq", 2))
+        elif name == "ide":
+            wait(A, K("pi"))
+            fin(A.activation(T.neg[:], T.pi[:, 0:128], COPY, scale=-0.25), K("id", 2))
+            fin(A.activation(T.ident[:], T.pi[:, 0:128], COPY, scale=0.25), K("id", 2))
+        elif name == "n0":
+            wait(V, k_n)
+            fin(V.tensor_scalar(T.n32[:], T.nraw[:], H - 1, None, AluOpType.bitwise_and), k_n0)
+            fin(V.tensor_scalar(T.kc0[:, 0:1], T.nraw[:, 0:1], 3 * H, None, AluOpType.bitwise_and), k_kc0)
+        elif name == "c0":
+            wait(V, k_n0, k_kc0)
+            fin(V.tensor_scalar(T.n32[hi, :], T.n32[hi, :], float(H), None, ADD), K("n32"))
+            fin(V.tensor_scalar(T.kc[lo, 0:1], T.kc0[lo, 0:1], -2.0, float(4 * H + R - 1), MUL, ADD), K("kc", 2))
+            fin(V.tensor_scalar(T.kc[hi, 0:1], T.kc0[hi, 0:1], -2.0, float(3 * H + R - 1), MUL, ADD), K("kc", 2))
+        elif name == "c1":
+            wait(V, k_v3)
+            fin(V.tensor_scalar(T.selg[0:8, :], T.v3[0:8, :], 0.0, None, AluOpType.is_equal), K("selg"))
+        elif name == "h0":
+            wait(V, K("ab"))
+            fin(V.tensor_copy(T.abf[0:8, :], T.ab32[0:8, :]), K("abf"))
+            wait(PE, K("selg"), K("abf"))
+            fin(PE.matmul(T.pab[:, 0:8], T.selg[0:8, :], T.abf[0:8, :], True, True), K("pab"))
+        elif name == "h1":
+            wait(V, K("pab"), K("n32"))
+            for j, r in enumerate((mate, rank)):
+                fin(V.tensor_scalar(T.raw[:, j:128:2] if MERGED else T.raw[:, 64 * j:64 * j + 64], T.n32[:], T.pab[:, 2 * r:2 * r + 1],
+                                    T.pab[:, 2 * r + 1:2 * r + 2], MUL, ADD), K("raw", 2))
+        elif name == "h2":
+            wait(V, K("raw", 2))
+            fin(V.tensor_scalar(T.u32[:], T.raw[:], 2, 1023, AluOpType.arith_shift_right, AluOpType.bitwise_and),
+                K("u"))
+        elif name == "h3":
+            wait(V, K("u"))
+            fin(V.tensor_scalar(T.uf[:], T.u32[:], 1.0 / 1024, None, MUL), K("uf"))
+        elif name == "cf":
+            wait(V, k_call, K("cnt"), k_pad)
+            fin(V.tensor_scalar(T.cf2[lo, 0:12], T.call[mine, 4:16], 0.5, None, MUL), K("cf", 2))
+            fin(V.tensor_scalar(T.cf2[hi, 0:12], T.call[mine, 2:14], 0.5, None, MUL), K("cf", 2))
+            scaled = "sq" in PRE_A
+            wait(PE, K("m", 5), K("eq", 4), K("cf", 2), K("raw", 2))
+            even, odd = T.cf2[:, 4:12:2], T.cf2[:, 5:12:2]
+            if scaled:
+                wait(PE, K("sq", 2))
+            o = T.pab[:, 8:9]
+            for j, (m, c) in enumerate(((0, 10), (0, 6), (1, 11), (1, 7))):
+                ins = PE.matmul(o, ((T.s0q, T.s1q) if scaled else (T.s0, T.s1))[m][:], T.cf2[:, c:c + 1], j == 0, j == 3)
+            fin(ins, K("size"))
+            o = T.pbef[:, 0:3]
+            PE.matmul(o, T.s0[:], T.cf2[:, 4:10:2], True, False)
+            PE.matmul(o, T.s0[:], T.cf2[:, 0:6:2], False, False)
+            PE.matmul(o, T.s1[:], T.cf2[:, 5:10:2], False, False)
+            PE.matmul(o, T.s1[:], T.cf2[:, 1:6:2], False, False)
+            PE.matmul(o, T.mq[:], T.cf2[:, 6:12:2], False, False)
+            fin(PE.matmul(o, T.mq[:], T.cf2[:, 7:12:2], False, True), K("bef"))
+            o = T.pd[:, 0:4]
+            PE.matmul(o, T.mq[:], even, True, False)
+            PE.matmul(o, T.mq[:], odd, False, False)
+            PE.matmul(o, T.ma[:], even, False, False)
+            fin(PE.matmul(o, T.mc[:], odd, False, True), K("d"))
+        elif name == "mem":
+            src, k = (T.u32, K("u")) if "sq" in PRE_A else (T.uf, K("uf"))
+            wait(V, K("size"), k)
+            fin(V.tensor_scalar(T.mem[:], src[:], T.pab[:, 8:9], 2047.5 - 1.0 / 2048, MUL, ADD), K("mem"))
+            if "add" not in PRE_V:
+                wait(PE, K("mem"), K("id", 2))
+                PE.matmul(T.po[:, 0:128], T.neg[:], T.mem[:], True, False)
+        elif name == "cmp" and "add" in PRE_V:
+            wait(V, K("mem"), K("bef"), K("d"))
+            for j, out in ((1, T.pt[:, 0:128]), (2, T.t2[:]), (3, T.pt[:, 128:256])):
+                fin(V.tensor_scalar(out, T.mem[:], T.pbef[:, j - 1:j], T.pd[:, j:j + 1], AluOpType.is_lt, MUL),
+                    K("cmp", 3))
+        elif name == "add":
+            wait(V, K("cmp", 3))
+            fin(V.tensor_tensor(T.pt[:, 0:128], T.pt[:, 0:128], T.t2[:], ADD), K("add", 2))
+            fin(V.tensor_tensor(T.t1[:], T.pt[:, 128:256], T.mem[:], SUB), K("add", 2))
+        elif name == "sum":
+            wait(V, K("add", 2))
+            fin(V.tensor_tensor(T.po[:, 0:128], T.pt[:, 0:128], T.t1[:], ADD), K("sum"))
+        elif name == "cmp":
+            wait(V, K("mem"), K("bef"), K("d"))
+            for j, out in ((1, T.t1), (2, T.t2), (3, T.t3)):
+                fin(V.tensor_scalar(out[:], T.mem[:], T.pbef[:, j - 1:j], T.pd[:, j:j + 1], AluOpType.is_lt, MUL),
+                    K("cmp%d" % j))
+                wait(PE, K("cmp%d" % j))
+                ins = PE.matmul(T.po[:, 0:128], T.ident[:], out[:], False, j == 3)
+            fin(ins, K("sum"))
+        elif name == "off":
+            wait(V, K("sum"), K("kc", 2))
+            fin(V.tensor_scalar(T.off[:], T.po[:, 0:128], T.pd[:, 0:1], T.kc[:, 0:1], ADD, ADD), K("off"))
+        else:
+            raise ValueError(name)
 
+    for q, names in ((V, PRE_V), (A, PRE_A), (SY, PRE_S)):
+        for name in names.split():
+            pre(q, name)
+
+    c = lcol(rank)
     eb = common(rank, [mate, far_other])
     for k, (a, _, b) in enumerate(CH_B):
         wait(g, k_sb[k])
-        src = T.bufb[:, a:b]
-        to = big[:, lcol(rank) + a:lcol(rank) + b]
-        sem = T.sem["p%d_%d" % (rank, k)]
         g.remote_dma_fused([
-            RemoteDMATransfer(dst_ids=[dst(far_other)], dma_engine_mask=_bits(eb[0::2]), remote_sem=sem, src=src, dst=to),
-            RemoteDMATransfer(dst_ids=[dst(mate)], dma_engine_mask=_bits(eb[1::2]), remote_sem=sem, src=src, dst=to),
-        ], local_sem=T.sem.sent)
+            RemoteDMATransfer(dst_ids=[dst(who_is[p])], dma_engine_mask=_bits(es), remote_sem=T.sem["p%s%d" % (p, k)],
+                              src=T.bufb[:, a:b], dst=big[:, c + a:c + b])
+            for p, es in (("F", eb[0::2]), ("M", eb[1::2]))], local_sem=T.sem.sent)
         sent[1] += len(eb)
     ea = common(rank, [far_same])
     for k, (a, _, b) in enumerate(CH_A):
         wait(g, k_sa[k])
-        ap = big[:, lcol(rank) + a:lcol(rank) + b]
         ad = topo.addr(cores[far_same])
-        g.remote_dma(ap, ap, T.sem["p%d_%d" % (rank, k)], T.sem.sent, ad[1], ad[0], _bits(ea))
+        g.remote_dma(big[:, c + a:c + b], big[:, c + a:c + b],
+                     T.sem["pS%d" % k], T.sem.sent, ad[1], ad[0], _bits(ea))
         sent[1] += len(ea)
-    k_go = tok()
-    g.sem_inc(k_go[0], 1)
-    k_go[1] = 1
-
-    def piece(s, k):
-        if s == far_same:
-            return [T.sem["p%d_%d" % (s, k)], len(common(s, [rank]))]
-        ss = common(s, [rank, far_same])
-        return [T.sem["p%d_%d" % (s, k)], len(ss[1::2] if s == mate else ss[0::2])]
-
-    k_w = tok()
-    k_dma = tok()
-
-    def cross(q, s, up, a, b):
-        if up:
-            o, i = big[hi, zcol(s) + a:zcol(s) + b], big[lo, lcol(s) + a:lcol(s) + b]
-        else:
-            o, i = big[lo, zcol(s + 1) + a:zcol(s + 1) + b], big[hi, lcol(s) + a:lcol(s) + b]
-        if q == "v":
-            mark(V.tensor_copy(o, i), k_w)
-        elif q == "a":
-            mark(A.activation(o, i, COPY), k_w)
-        else:
-            mark(SY.dma_start(o, i), k_dma, 16)
-
-    wait(SY, *(k_sb + k_sa + [k_go]))
-    cross("s", rank, True, 0, H)
-    cross("s", rank, False, 0, H)
-    wait(SY, piece(mate, 0), piece(mate, 1))
-    cross("s", mate, True, 0, H)
-    cross("s", mate, False, 0, H)
-    far = [(far_other, k, ch) for k, ch in enumerate(CH_B)] + [(far_same, k, ch) for k, ch in enumerate(CH_A)]
-    wait(A, *(k_sb + k_sa))
-    for s, k, ch in far:
-        wait(A, piece(s, k))
-        cross("a", s, True, ch[0], ch[2])
-
-    def down(i):
-        s, k, ch = far[i]
-        wait(V, piece(s, k))
-        cross("v", s, False, ch[0], ch[2])
-
-    wait(PE, k_m, k_cf)
-    PE.matmul(T.pbef[:, 0:4], T.s0[:], T.cf2[:, 4:12:2], True, False)
-    PE.matmul(T.pbef[:, 0:4], T.s0[:], T.cf2[:, 0:8:2], False, False)
-    PE.matmul(T.pbef[:, 0:4], T.s1[:], T.cf2[:, 5:12:2], False, False)
-    k_bef = mark(PE.matmul(T.pbef[:, 0:4], T.s1[:], T.cf2[:, 1:8:2], False, True))
-    PE.matmul(T.pd[:, 0:4], T.ma[:], T.cf2[:, 4:12:2], True, False)
-    k_d = mark(PE.matmul(T.pd[:, 0:4], T.mc[:], T.cf2[:, 5:12:2], False, True))
-    wait(V, k_bef, k_uf)
-    k_mem = mark(V.tensor_scalar(T.mem[:], T.uf[:], T.pbef[:, 3:4], -0.5 + 1.0 / 2048, MUL, ADD))
-    wait(V, k_mem, k_d)
-    k_t = tok()
-    for q, out in ((1, T.pt[:, 0:128]), (2, T.t2[:]), (3, T.pt[:, 128:256])):
-        mark(V.tensor_scalar(out, T.mem[:], T.pbef[:, q - 1:q], T.pd[:, q:q + 1], AluOpType.is_ge, MUL), k_t)
-    wait(V, *(k_sb + k_sa))
-    down(0)
-    wait(V, k_t)
-    k_s = mark(V.tensor_tensor(T.pt[:, 0:128], T.pt[:, 0:128], T.t2[:], ADD))
-    mark(V.tensor_tensor(T.tb[:], T.pt[:, 128:256], T.mem[:], ADD), k_s)
-    down(1)
-    wait(V, k_s)
-    k_c = mark(V.tensor_tensor(T.tc[:], T.pt[:, 0:128], T.tb[:], ADD))
-    down(2)
-    wait(V, k_c, k_kc, k_fill)
-    k_off = mark(V.tensor_scalar(T.off[:], T.tc[:], T.pd[:, 0:1], T.kc[:, 0:1], ADD, ADD))
-    down(3)
+    if "go" in PRE_S:
+        g.sem_inc(K("go")[0], 1)
 
     win = big[:, W0:W0 + 9 * H]
-    wait(V, k_off, k_dma, k_w)
-    wait(A, k_off, k_dma, k_w)
+    for q in (V, A):
+        wait(q, K("off"), k_w)
+        if k_dma[1]:
+            wait(q, k_dma)
+    zout = (T.pz0[:, 0:256], T.pz1[:, 0:256], T.zs[:, 0:256], T.zs[:, 256:512])
+    pl = T.pt[:, 256:512]
 
-    def draw(who, second, b):
-        c = 64 * who + 32 * second + 16 * b
-        return win.indirect(T.off[:, c:c + 16])
+    def draw(q, name):
+        k = K("draw" + name)
+        if name[0] in "fda":
+            j = int(name[1])
+            c = 256 * j
+            if name[0] == "f":
+                src = win.indirect(T.off[:, 16 * j:16 * j + 16])
+                fin(V.tensor_copy(T.vb[:, c:c + 256], src) if q is V else A.activation(T.vb[:, c:c + 256], src, COPY), k)
+            elif name[0] == "d":
+                wait(V, K("drawf%d" % j))
+                fin(V.tensor_tensor(T.dd[:, c:c + 256], win.indirect(T.off[:, 64 + 16 * j:80 + 16 * j]),
+                                    T.vb[:, c:c + 256], SUB), k)
+            else:
+                wait(A, K("drawd%d" % j))
+                fin(A.activation(zout[j], T.dd[:, c:c + 256], ABS), k)
+        elif name[0] == "1":
+            j = "ab".index(name[1])
+            wait(V, K("drawa%d" % j), K("drawa%d" % (j + 2)))
+            fin(V.tensor_tensor((pl, T.l1[:])[j], zout[j], zout[j + 2], ADD), k)
+        elif name == "2":
+            wait(V, K("draw1a"), K("draw1b"))
+            fin(V.tensor_tensor(T.l2[:], pl, T.l1[:], ADD), k)
+        else:
+            i = int(name)
+            src, out = {3: (T.l2, T.l3), 4: (T.l3, T.l4), 5: (T.l4, T.res)}[i]
+            m = 1024 >> i
+            wait(V, K("draw%d" % (i - 1)))
+            fin(V.tensor_tensor(out[:], src[:, 0:m], src[:, m:2 * m], ADD), k)
 
-    def blk(buf, who, b):
-        c = 512 * who + 256 * b
-        return buf[:, c:c + 256]
-
-    pz = (T.pz0, T.pz1)
-    k_z = [tok(), tok()]
-
-    def first(q, who, b):
-        if q == "a":
-            return mark(A.activation(blk(T.vb, who, b), draw(who, 0, b), COPY))
-        return mark(V.tensor_copy(blk(T.vb, who, b), draw(who, 0, b)))
-
-    def diff(k, who, b):
-        wait(V, k)
-        return mark(V.tensor_tensor(blk(T.dd, who, b), draw(who, 1, b), blk(T.vb, who, b), SUB))
-
-    def size(k, who, b):
-        wait(A, k)
-        out = pz[who][:, 0:256] if b == 0 else T.zs[:, 256 * who:256 * who + 256]
-        mark(A.activation(out, blk(T.dd, who, b), ABS), k_z[who])
-
-    def level(i, who, k):
-        c, d, f = 128 * who, 64 * who, 32 * who
-        wait(V, k)
+    def draw2(q, name):
+        k = K("draw" + name, 2 if name in ("M1", "O1") + TWO else 1)
+        if name[0] in "fda":
+            j = int(name[1])
+            c, lst = 256 * j, 64 * (j // 2) + 16 * (j % 2)
+            if name[0] == "f":
+                src = win.indirect(T.off[:, lst:lst + 16])
+                fin(V.tensor_copy(T.vb[:, c:c + 256], src) if q is V else A.activation(T.vb[:, c:c + 256], src, COPY), k)
+            elif name[0] == "d":
+                wait(V, K("drawf%d" % j))
+                fin(V.tensor_tensor(T.dd[:, c:c + 256], win.indirect(T.off[:, lst + 32:lst + 48]),
+                                    T.vb[:, c:c + 256], SUB), k)
+            else:
+                wait(A, K("drawd%d" % j))
+                fin(A.activation(zout[2 * (j % 2) + j // 2], T.dd[:, c:c + 256], ABS), k)
+            return
+        who, i = "MO".index(name[0]), int(name[1])
+        m = 512 >> i
         if i == 1:
-            k = mark(V.tensor_tensor(T.pl[:, c:c + 128], pz[who][:, 0:128], T.zs[:, 2 * c:2 * c + 128], ADD))
-            return mark(V.tensor_tensor(T.l1[:, c:c + 128], pz[who][:, 128:256], T.zs[:, 2 * c + 128:2 * c + 256], ADD), k)
-        if i == 2:
-            return mark(V.tensor_tensor(T.l2[:, c:c + 128], T.pl[:, c:c + 128], T.l1[:, c:c + 128], ADD))
-        if i == 3:
-            return mark(V.tensor_tensor(T.l3[:, d:d + 64], T.l2[:, c:c + 64], T.l2[:, c + 64:c + 128], ADD))
-        if i == 4:
-            return mark(V.tensor_tensor(T.l4[:, f:f + 32], T.l3[:, d:d + 32], T.l3[:, d + 32:d + 64], ADD))
-        res = (T.resm, T.reso)[who]
-        k = tok()
-        for h in range(2):
-            mark(V.tensor_tensor(res[lo, 16 * h:16 * h + 16], T.l4[half[h], f:f + 16], T.l4[half[h], f + 16:f + 32], ADD), k)
-        return k
+            k = K("draw" + name, 2)
+            wait(V, K("drawa%d" % (2 * who)), K("drawa%d" % (2 * who + 1)))
+            for a, out in ((0, pl), (128, T.l1)):
+                fin(V.tensor_tensor(out[:, 128 * who:128 * who + 128] if a else T.pt[:, 256 + 128 * who:384 + 128 * who],
+                                    (T.pz0, T.pz1)[who][:, a:a + 128], T.zs[:, 256 * who + a:256 * who + a + 128], ADD), k)
+        elif i == 2:
+            wait(V, K("draw%s1" % name[0], 2))
+            fin(V.tensor_tensor(T.l2[:, m * who:m * who + m], T.pt[:, 256 + m * who:256 + m * who + m],
+                                T.l1[:, m * who:m * who + m], ADD), k)
+        else:
+            src, out = {3: (T.l2, T.l3), 4: (T.l3, T.l4), 5: (T.l4, T.res)}[i]
+            c = 2 * m * who
+            wait(V, K("draw%s%d" % (name[0], i - 1)))
+            if name in TWO:
+                out = T.l4m if who == 0 else T.res
+                wait(V, k_fill)
+                for h in range(2):
+                    fin(V.tensor_tensor(out[lo, m * h:m * h + m], src[half[h], c:c + m],
+                                        src[half[h], c + m:c + 2 * m], ADD), k)
+                return
+            fin(V.tensor_tensor(out[:, m * who:m * who + m], src[:, c:c + m], src[:, c + m:c + 2 * m], ADD), k)
 
-    v00 = first("a", 0, 0)
-    v01 = first("v", 0, 1)
-    v10 = first("a", 1, 0)
-    d00 = diff(v00, 0, 0)
-    size(d00, 0, 0)
-    d01 = diff(v01, 0, 1)
-    size(d01, 0, 1)
-    v11 = first("a", 1, 1)
-    d10 = diff(v10, 1, 0)
-    size(d10, 1, 0)
-    km = level(1, 0, k_z[0])
-    d11 = diff(v11, 1, 1)
-    size(d11, 1, 1)
-    km = level(2, 0, km)
-    km = level(3, 0, km)
-    km = level(4, 0, km)
-    ko = level(1, 1, k_z[1])
-    k_resm = level(5, 0, km)
-    for i in (2, 3, 4, 5):
-        ko = level(i, 1, ko)
-    k_reso = ko
+    for q, names in ((V, DRAW_V), (A, DRAW_A)):
+        for name in names.split():
+            (draw if MERGED else draw2)(q, name)
 
-    wait(g, k_resm)
-    ad = topo.addr(cores[mate])
     er = common(rank, [mate])
-    g.remote_dma(T.land[:], T.resm[:], T.sem.res, T.sem.sent, ad[1], ad[0], _bits(er))
+    if not MERGED:
+        named["draw5"] = K("drawO5")
+        wait(g, K("drawM4"))
+        tr = RemoteDMATransfer(dst_ids=[dst(mate)], dma_engine_mask=_bits(er), remote_sem=T.sem.res,
+                               srcs=[T.l4[:, 0:16], T.l4[:, 16:32]], dsts=[T.land[:]], alu_op=1)
+        if "M4" in TWO:
+            tr = RemoteDMATransfer(dst_ids=[dst(mate)], dma_engine_mask=_bits(er), remote_sem=T.sem.res,
+                                   srcs=[T.l4m[:, 0:48], T.l4m[:, 16:64]], dsts=[T.land3[:]], alu_op=1)
+    elif FOLD:
+        wait(g, K("draw4"))
+        tr = RemoteDMATransfer(dst_ids=[dst(mate)], dma_engine_mask=_bits(er), remote_sem=T.sem.res,
+                               srcs=[T.l4[:, 0:16], T.l4[:, 32:48]], dsts=[T.land[:]], alu_op=1)
+    else:
+        wait(g, K("draw5"))
+        tr = RemoteDMATransfer(dst_ids=[dst(mate)], dma_engine_mask=_bits(er), remote_sem=T.sem.res,
+                               src=T.res[:, 0:16], dst=T.land[:])
+    g.remote_dma_fused([tr], local_sem=T.sem.sent)
     sent[1] += len(er)
-    wait(A, k_reso)
-    k_y0 = mark(A.dma_start(T.y[mine, :], T.reso[lo, :]), by=16)
-    wait(SY, [T.sem.res, len(common(mate, [rank]))])
-    k_y1 = mark(SY.dma_start(T.y[theirs, :], T.land[lo, :]), by=16)
-    wait(A, k_y0)
-    wait(SY, k_y1)
+    k_land = [T.sem.res, len(common(mate, [rank])), "res"]
+    stores = {SY_: [] for SY_ in range(2)}
+    if "O5" in TWO:
+        stores[1].append((K("draw5"), T.y[mine, :], T.res[lo, :]))
+    else:
+        for h in range(2):
+            stores[h].append((K("draw5"), T.y[mine, 16 * h:16 * h + 16], T.res[half[h], 16:32]))
+    if "M4" in TWO:
+        stores[0].append((k_land, T.y[theirs, :], T.land3[lo, 0:3:2, :]))
+    else:
+        for h in range(2):
+            stores[0 if "O5" in TWO else h].append((k_land, T.y[theirs, 16 * h:16 * h + 16], T.land[half[h], :]))
+    for h, q in enumerate((SY, A)):
+        k = tok()
+        for kk, o, i in stores[h]:
+            wait(q, kk)
+            mark(q.dma_start(o, i), k, 16)
+        wait(q, k)
     wait(g, sent)

from concourse.bass import DstId, RemoteDMATransfer
from concourse.mybir import AluOpType, ActivationFunctionType

R = 2048
H = R // 2
CH_B = [(0, 256, 512), (512, 640, 1024)]
CH_A = [(0, 256, 512), (512, 768, 1024)]
W0 = H
XA0 = 9 * H
LOAD_S = "cnt xb0 ab xa0 xa1"
LOAD_A = "idx xb1"
IOTA = "vv n v3"
IOTA2 = ""
PRE_V = "eq n0 c0 ob c1 oa h0 sB0 h1 sB1 h2 sA0 cf sA1 mem Fd0 cmp Fd1 add Sd0 sum Sd1 off"
PRE_A = "sg0 sg1 sq sB0 sB1 sA0 sA1 Fu0 Fu1 Su0 Su1"
PRE_S = "Ou Od Mu Md"
DRAW_V = "f1 d0 d1 d2 d3 M1 M2 M3 O1 M4 O2 O3 O4 O5"
DRAW_A = "f0 f2 f3 a0 a1 a2 a3"
FOLD = True
MERGED = False
TWO = ("M4", "O5")

F32, BF, I32, U16, F16 = "float32", "bfloat16", "int32", "uint16", "float16"
SCRATCH = {
    "big": ("sbuf", [128, 11 * H], BF), "bufb": ("sbuf", [128, H], BF),
    "idx32": ("sbuf", [128, 128], I32), "offb": ("sbuf", [128, 64], U16), "offa": ("sbuf", [128, 64], U16),
    "call": ("sbuf", [128, 16], I32), "ab32": ("sbuf", [128, 8], I32), "abf": ("sbuf", [128, 8], F32),
    "nraw": ("sbuf", [128, 64], I32), "n32": ("sbuf", [128, 64], I32),
    "kc0": ("sbuf", [128, 4], I32), "kc": ("sbuf", [128, 4], F32),
    "v3": ("sbuf", [128, 128], BF), "selg": ("sbuf", [128, 128], F32), "vv": ("sbuf", [128, 128], BF),
    "ma": ("sbuf", [128, 128], BF), "mc": ("sbuf", [128, 128], BF), "mq": ("sbuf", [128, 128], BF),
    "s0": ("sbuf", [128, 128], BF), "s1": ("sbuf", [128, 128], BF),
    "raw": ("sbuf", [128, 128], I32), "u32": ("sbuf", [128, 128], I32), "uf": ("sbuf", [128, 128], F32),
    "mem": ("sbuf", [128, 128], F16), "t1": ("sbuf", [128, 128], F32), "t2": ("sbuf", [128, 128], F32),
    "s0q": ("sbuf", [128, 128], BF), "s1q": ("sbuf", [128, 128], BF),
    "neg": ("sbuf", [128, 128], BF), "ident": ("sbuf", [128, 128], F32),
    "pi": ("psum", [128, 512], F32), "po": ("psum", [128, 512], F32),
    "t3": ("sbuf", [128, 128], F32), "off": ("sbuf", [128, 128], U16), "cf2": ("sbuf", [128, 16], F16),
    "vb": ("sbuf", [128, 1024], BF), "dd": ("sbuf", [128, 1024], F32), "zs": ("sbuf", [128, 512], F32),
    "l1": ("sbuf", [128, 256], F32), "l2": ("sbuf", [128, 256], F32), "l3": ("sbuf", [128, 128], F32),
    "l4": ("sbuf", [128, 64], F32), "res": ("sbuf", [128, 32], F32), "land": ("sbuf", [128, 16], F32),
    "l4m": ("sbuf", [128, 64], F32), "land3": ("sbuf", [128, 3, 16], F32),
    "pab": ("psum", [128, 512], F32), "pbef": ("psum", [128, 512], F32), "pd": ("psum", [128, 512], F32),
    "pt": ("psum", [128, 512], F32), "pz0": ("psum", [128, 512], F32), "pz1": ("psum", [128, 512], F32),
}
NLOCAL = 90
SEMAPHORES = (["cnt", "res", "sent"] + ["p%s%d" % (q, k) for q in "MFS" for k in range(4)]
              + ["k%d" % i for i in range(NLOCAL)])

ADD, SUB, MUL = AluOpType.add, AluOpType.subtract, AluOpType.mult
COPY, ABS = ActivationFunctionType.Copy, ActivationFunctionType.Abs
SIGN, IDENT = ActivationFunctionType.Sign, ActivationFunctionType.Identity


def _bits(engines):
    m = 0
    for e in engines:
        m |= 1 << e
    return m


def rank_program(g, core, T, topo):
    rank = T.rank_of(core)
    if rank is None:
        return
    cores = list(T.cores)
    n = len(cores)
    order = sorted(range(n), key=lambda r: (topo.chip(cores[r]), topo.die(cores[r]), r))
    place = {r: i for i, r in enumerate(order)}
    t = place[rank] % 2
    pair = [order[place[rank] - t], order[place[rank] - t + 1]]
    mate = pair[1 - t]
    far_same = [r for r in range(n) if r not in pair and place[r] % 2 == t][0]
    far_other = [r for r in range(n) if r not in pair and place[r] % 2 != t][0]
    others = [r for r in range(n) if r != rank]
    who_is = {"O": rank, "M": mate, "F": far_other, "S": far_same}
    chunks = {"O": CH_A, "S": CH_A, "M": CH_B, "F": CH_B, "A": CH_A, "B": CH_B}

    def dst(r):
        a = topo.addr(cores[r])
        return DstId(rid=a[0], pnc=a[1])

    def common(src, rs):
        return [e for e in topo.engines(cores[src], cores[rs[0]])
                if all(e in topo.engines(cores[src], cores[r]) for r in rs)]

    V, A, PE, SY = g.vector, g.scalar, g.tensor, g.sync
    queues = [V, A, PE, SY, g]
    used = [0]

    def tok(total=0):
        used[0] += 1
        return [T.sem["k%d" % (used[0] - 1)], total, "k%d" % used[0]]

    def mark(ins, k=None, by=1):
        if k is None:
            k = tok()
        ins.then_inc(k[0], by)
        k[1] += by
        return k

    named = {}

    def K(name, total=1):
        if name not in named:
            named[name] = tok(total)
        return named[name]

    def fin(ins, k, by=1):
        ins.then_inc(k[0], by)

    seen = {}

    def wait(q, *ks):
        for k in ks:
            key = (queues.index(q), k[2])
            if seen.get(key, 0) < k[1]:
                seen[key] = k[1]
                q.wait_ge(k[0], k[1])

    lo, hi = slice(0, 64), slice(64, 128)
    half = (lo, hi)
    mine, theirs = half[t], half[1 - t]
    big = T.big

    def lcol(r):
        return R + R * r

    mycnt = T.call[:, 8 + 2 * rank:10 + 2 * rank]
    loads = {"cnt": (mycnt, T.counts[:], K("cnt", 16)), "idx": (T.idx32[:], T.idx[:], K("idx", 16)),
             "ab": (T.ab32[0:8, :], T.ab[:], K("ab", 16))}
    for h in range(2):
        loads["xb%d" % h] = (big[half[h], 0:R], T.x[theirs, :], K("xb", 32))
        loads["xa%d" % h] = (big[half[h], XA0:XA0 + R], T.x[mine, :], K("xa", 32))
    for q, names in ((SY, LOAD_S), (A, LOAD_A)):
        for name in names.split():
            o, i, k = loads[name]
            fin(q.dma_start(o, i), k, 16)

    k_n, k_v3, k_vv = K("n"), K("v3"), [K("vv")] * 2
    vv_pat = [[-16, 2], [-32, 4], [-1, 16]]
    def iotas(names):
        for name in names.split():
            if name == "n":
                fin(g.iota(T.nraw[:], [[1, 2], [2, 32]], 0, 64), k_n)
            elif name == "v3":
                fin(g.iota(T.v3[0:8, :], [[0, 2], [-1, 4], [0, 16]], -4 * t, 1, allow_small_or_imprecise_dtypes=True),
                    k_v3)
            else:
                fin(g.iota(T.vv[:], vv_pat, 0, 2, allow_small_or_imprecise_dtypes=True), k_vv[0])

    iotas(IOTA)

    k_pad = mark(V.memset(T.call[:, 0:8], 0))
    k_fill = mark(V.memset(T.l4m[hi, :], 0.0)) if "M4" in TWO else k_pad
    k_n0, k_kc0 = K("n0"), K("kc0")

    sent = [T.sem.sent, 0, "sent"]
    wait(g, K("cnt"))
    e = common(rank, others)
    g.remote_dma_fused([RemoteDMATransfer(dst_ids=[dst(r) for r in others], dma_engine_mask=_bits(e),
                                          remote_sem=T.sem.cnt, srcs=[mycnt], dsts=[mycnt] * len(others))],
                       local_sem=T.sem.sent)
    sent[1] += len(e)
    k_call = [T.sem.cnt, sum(len(common(s, [r for r in range(n) if r != s])) for s in others), "cnt"]
    iotas(IOTA2)

    def sorted_(p, k):
        a, m, b = chunks[p][k]
        return K("s%s%d" % (p, k), (m > a) + (b > m))

    k_sb = [sorted_("B", k) for k in range(len(CH_B))]
    k_sa = [sorted_("A", k) for k in range(len(CH_A))]

    def piece(p, k):
        if p == "O":
            return k_sa[k]
        name = "p%s%d" % (p, k)
        if p == "S":
            return [T.sem[name], len(common(far_same, [rank])), name]
        ss = common(who_is[p], [rank, far_same])
        return [T.sem[name], len(ss[1::2] if p == "M" else ss[0::2]), name]

    k_w, k_dma = tok(), tok()

    def pre(q, name):
        if name[0] == "s" and name[1] in "AB":
            p, k = name[1], int(name[2])
            a, m, b = chunks[p][k]
            a, b = (a, m) if q is V else (m, b)
            win, offs, out, o = ((big[:, 0:R], T.offb, T.bufb, 0) if p == "B"
                                 else (big[:, XA0:XA0 + R], T.offa, big, lcol(rank)))
            wait(q, K("x" + p.lower()), K("o" + p.lower(), 2))
            src = win.indirect(offs[:, a // 16:b // 16])
            fin(V.tensor_copy(out[:, o + a:o + b], src) if q is V else A.activation(out[:, o + a:o + b], src, COPY),
                sorted_(p, k))
        elif name[0] in who_is:
            p, up = name[0], name[1] == "u"
            a, b = (512 * int(name[2]), 512 * int(name[2]) + 512) if name[2:] else (0, H)
            ks = [k for k, ch in enumerate(chunks[p]) if ch[0] < b and a < ch[2]]
            wait(q, *[piece(p, k) for k in ks])
            if up and who_is[p] == 0:
                wait(q, *k_sb)
            if not up and who_is[p] == n - 1:
                wait(q, *k_sa)
            c = lcol(who_is[p])
            o, i = ((big[hi, c - H + a:c - H + b], big[lo, c + a:c + b]) if up
                    else (big[lo, c + H + a:c + H + b], big[hi, c + a:c + b]))
            if q is V:
                mark(V.tensor_copy(o, i), k_w)
            elif q is A:
                mark(A.activation(o, i, COPY), k_w)
            else:
                mark(SY.dma_start(o, i), k_dma, 16)
        elif name == "go":
            wait(q, K("go"))
        elif name in ("ob", "oa"):
            wait(V, K("idx"))
            buf, part = (T.offb, theirs) if name == "ob" else (T.offa, mine)
            for h in range(2):
                fin(V.tensor_copy(buf[half[h], :], T.idx32[part, 64 * h:64 * h + 64]), K(name, 2))
        elif name == "sg0":
            wait(A, k_vv[0])
            fin(A.activation(T.ma[lo, :], T.vv[lo, :], SIGN, bias=-0.5, scale=-1.0), K("m", 5))
            fin(A.activation(T.mc[lo, :], T.vv[lo, :], SIGN, bias=-1.5, scale=-1.0), K("m", 5))
        elif name == "sg1":
            wait(A, k_vv[1])
            fin(A.activation(T.ma[hi, :], T.vv[hi, :], SIGN, bias=-128.5), K("m", 5))
            fin(A.activation(T.mc[hi, :], T.vv[hi, :], SIGN, bias=-127.5), K("m", 5))
            fin(A.activation(T.mq[:], T.vv[:], IDENT, bias=0.25, scale=0.0), K("m", 5))
        elif name == "eq":
            wait(V, *k_vv)
            for buf, c in ((T.s0, 0.0), (T.s1, -1.0)):
                for h in range(2):
                    fin(V.tensor_scalar(buf[half[h], :], T.vv[half[h], :], c + 128.0 * h, -2.0, AluOpType.is_equal,
                                        MUL), K("eq", 4))
            if "ide" in PRE_A:
                wait(PE, K("eq", 4))
                PE.matmul(T.pi[:, 0:128], T.s0[lo, :], T.s0[lo, :], True, False)
                fin(PE.matmul(T.pi[:, 0:128], T.s1[lo, :], T.s1[lo, :], False, True), K("pi"))
        elif name == "sq":
            wait(A, K("eq", 4))
            fin(A.activation(T.s0q[:], T.s0[:], COPY, scale=1.0 / 1024), K("sq", 2))
            fin(A.activation(T.s1q[:], T.s1[:], COPY, scale=1.0 / 1024), K("sq", 2))
        elif name == "ide":
            wait(A, K("pi"))
            fin(A.activation(T.neg[:], T.pi[:, 0:128], COPY, scale=-0.25), K("id", 2))
            fin(A.activation(T.ident[:], T.pi[:, 0:128], COPY, scale=0.25), K("id", 2))
        elif name == "n0":
            wait(V, k_n)
            fin(V.tensor_scalar(T.n32[:], T.nraw[:], H - 1, None, AluOpType.bitwise_and), k_n0)
            fin(V.tensor_scalar(T.kc0[:, 0:1], T.nraw[:, 0:1], 3 * H, None, AluOpType.bitwise_and), k_kc0)
        elif name == "c0":
            wait(V, k_n0, k_kc0)
            fin(V.tensor_scalar(T.n32[hi, :], T.n32[hi, :], float(H), None, ADD), K("n32"))
            fin(V.tensor_scalar(T.kc[lo, 0:1], T.kc0[lo, 0:1], -2.0, float(4 * H + R - 1), MUL, ADD), K("kc", 2))
            fin(V.tensor_scalar(T.kc[hi, 0:1], T.kc0[hi, 0:1], -2.0, float(3 * H + R - 1), MUL, ADD), K("kc", 2))
        elif name == "c1":
            wait(V, k_v3)
            fin(V.tensor_scalar(T.selg[0:8, :], T.v3[0:8, :], 0.0, None, AluOpType.is_equal), K("selg"))
        elif name == "h0":
            wait(V, K("ab"))
            fin(V.tensor_copy(T.abf[0:8, :], T.ab32[0:8, :]), K("abf"))
            wait(PE, K("selg"), K("abf"))
            fin(PE.matmul(T.pab[:, 0:8], T.selg[0:8, :], T.abf[0:8, :], True, True), K("pab"))
        elif name == "h1":
            wait(V, K("pab"), K("n32"))
            for j, r in enumerate((mate, rank)):
                fin(V.tensor_scalar(T.raw[:, j:128:2] if MERGED else T.raw[:, 64 * j:64 * j + 64], T.n32[:], T.pab[:, 2 * r:2 * r + 1],
                                    T.pab[:, 2 * r + 1:2 * r + 2], MUL, ADD), K("raw", 2))
        elif name == "h2":
            wait(V, K("raw", 2))
            fin(V.tensor_scalar(T.u32[:], T.raw[:], 2, 1023, AluOpType.arith_shift_right, AluOpType.bitwise_and),
                K("u"))
        elif name == "h3":
            wait(V, K("u"))
            fin(V.tensor_scalar(T.uf[:], T.u32[:], 1.0 / 1024, None, MUL), K("uf"))
        elif name == "cf":
            wait(V, k_call, K("cnt"), k_pad)
            fin(V.tensor_scalar(T.cf2[lo, 0:12], T.call[mine, 4:16], 0.5, None, MUL), K("cf", 2))
            fin(V.tensor_scalar(T.cf2[hi, 0:12], T.call[mine, 2:14], 0.5, None, MUL), K("cf", 2))
            scaled = "sq" in PRE_A
            wait(PE, K("m", 5), K("eq", 4), K("cf", 2), K("raw", 2))
            even, odd = T.cf2[:, 4:12:2], T.cf2[:, 5:12:2]
            if scaled:
                wait(PE, K("sq", 2))
            o = T.pab[:, 8:9]
            for j, (m, c) in enumerate(((0, 10), (0, 6), (1, 11), (1, 7))):
                ins = PE.matmul(o, ((T.s0q, T.s1q) if scaled else (T.s0, T.s1))[m][:], T.cf2[:, c:c + 1], j == 0, j == 3)
            fin(ins, K("size"))
            o = T.pbef[:, 0:3]
            PE.matmul(o, T.s0[:], T.cf2[:, 4:10:2], True, False)
            PE.matmul(o, T.s0[:], T.cf2[:, 0:6:2], False, False)
            PE.matmul(o, T.s1[:], T.cf2[:, 5:10:2], False, False)
            PE.matmul(o, T.s1[:], T.cf2[:, 1:6:2], False, False)
            PE.matmul(o, T.mq[:], T.cf2[:, 6:12:2], False, False)
            fin(PE.matmul(o, T.mq[:], T.cf2[:, 7:12:2], False, True), K("bef"))
            o = T.pd[:, 0:4]
            PE.matmul(o, T.mq[:], even, True, False)
            PE.matmul(o, T.mq[:], odd, False, False)
            PE.matmul(o, T.ma[:], even, False, False)
            fin(PE.matmul(o, T.mc[:], odd, False, True), K("d"))
        elif name == "mem":
            src, k = (T.u32, K("u")) if "sq" in PRE_A else (T.uf, K("uf"))
            wait(V, K("size"), k)
            fin(V.tensor_scalar(T.mem[:], src[:], T.pab[:, 8:9], 2047.5 - 1.0 / 2048, MUL, ADD), K("mem"))
            if "add" not in PRE_V:
                wait(PE, K("mem"), K("id", 2))
                PE.matmul(T.po[:, 0:128], T.neg[:], T.mem[:], True, False)
        elif name == "cmp" and "add" in PRE_V:
            wait(V, K("mem"), K("bef"), K("d"))
            for j, out in ((1, T.pt[:, 0:128]), (2, T.t2[:]), (3, T.pt[:, 128:256])):
                fin(V.tensor_scalar(out, T.mem[:], T.pbef[:, j - 1:j], T.pd[:, j:j + 1], AluOpType.is_lt, MUL),
                    K("cmp", 3))
        elif name == "add":
            wait(V, K("cmp", 3))
            fin(V.tensor_tensor(T.pt[:, 0:128], T.pt[:, 0:128], T.t2[:], ADD), K("add", 2))
            fin(V.tensor_tensor(T.t1[:], T.pt[:, 128:256], T.mem[:], SUB), K("add", 2))
        elif name == "sum":
            wait(V, K("add", 2))
            fin(V.tensor_tensor(T.po[:, 0:128], T.pt[:, 0:128], T.t1[:], ADD), K("sum"))
        elif name == "cmp":
            wait(V, K("mem"), K("bef"), K("d"))
            for j, out in ((1, T.t1), (2, T.t2), (3, T.t3)):
                fin(V.tensor_scalar(out[:], T.mem[:], T.pbef[:, j - 1:j], T.pd[:, j:j + 1], AluOpType.is_lt, MUL),
                    K("cmp%d" % j))
                wait(PE, K("cmp%d" % j))
                ins = PE.matmul(T.po[:, 0:128], T.ident[:], out[:], False, j == 3)
            fin(ins, K("sum"))
        elif name == "off":
            wait(V, K("sum"), K("kc", 2))
            fin(V.tensor_scalar(T.off[:], T.po[:, 0:128], T.pd[:, 0:1], T.kc[:, 0:1], ADD, ADD), K("off"))
        else:
            raise ValueError(name)

    for q, names in ((V, PRE_V), (A, PRE_A), (SY, PRE_S)):
        for name in names.split():
            pre(q, name)

    c = lcol(rank)
    eb = common(rank, [mate, far_other])
    for k, (a, _, b) in enumerate(CH_B):
        wait(g, k_sb[k])
        g.remote_dma_fused([
            RemoteDMATransfer(dst_ids=[dst(who_is[p])], dma_engine_mask=_bits(es), remote_sem=T.sem["p%s%d" % (p, k)],
                              src=T.bufb[:, a:b], dst=big[:, c + a:c + b])
            for p, es in (("F", eb[0::2]), ("M", eb[1::2]))], local_sem=T.sem.sent)
        sent[1] += len(eb)
    ea = common(rank, [far_same])
    for k, (a, _, b) in enumerate(CH_A):
        wait(g, k_sa[k])
        ad = topo.addr(cores[far_same])
        g.remote_dma(big[:, c + a:c + b], big[:, c + a:c + b],
                     T.sem["pS%d" % k], T.sem.sent, ad[1], ad[0], _bits(ea))
        sent[1] += len(ea)
    if "go" in PRE_S:
        g.sem_inc(K("go")[0], 1)

    win = big[:, W0:W0 + 9 * H]
    for q in (V, A):
        wait(q, K("off"), k_w)
        if k_dma[1]:
            wait(q, k_dma)
    zout = (T.pz0[:, 0:256], T.pz1[:, 0:256], T.zs[:, 0:256], T.zs[:, 256:512])
    pl = T.pt[:, 256:512]

    def draw(q, name):
        k = K("draw" + name)
        if name[0] in "fda":
            j = int(name[1])
            c = 256 * j
            if name[0] == "f":
                src = win.indirect(T.off[:, 16 * j:16 * j + 16])
                fin(V.tensor_copy(T.vb[:, c:c + 256], src) if q is V else A.activation(T.vb[:, c:c + 256], src, COPY), k)
            elif name[0] == "d":
                wait(V, K("drawf%d" % j))
                fin(V.tensor_tensor(T.dd[:, c:c + 256], win.indirect(T.off[:, 64 + 16 * j:80 + 16 * j]),
                                    T.vb[:, c:c + 256], SUB), k)
            else:
                wait(A, K("drawd%d" % j))
                fin(A.activation(zout[j], T.dd[:, c:c + 256], ABS), k)
        elif name[0] == "1":
            j = "ab".index(name[1])
            wait(V, K("drawa%d" % j), K("drawa%d" % (j + 2)))
            fin(V.tensor_tensor((pl, T.l1[:])[j], zout[j], zout[j + 2], ADD), k)
        elif name == "2":
            wait(V, K("draw1a"), K("draw1b"))
            fin(V.tensor_tensor(T.l2[:], pl, T.l1[:], ADD), k)
        else:
            i = int(name)
            src, out = {3: (T.l2, T.l3), 4: (T.l3, T.l4), 5: (T.l4, T.res)}[i]
            m = 1024 >> i
            wait(V, K("draw%d" % (i - 1)))
            fin(V.tensor_tensor(out[:], src[:, 0:m], src[:, m:2 * m], ADD), k)

    def draw2(q, name):
        k = K("draw" + name, 2 if name in ("M1", "O1") + TWO else 1)
        if name[0] in "fda":
            j = int(name[1])
            c, lst = 256 * j, 64 * (j // 2) + 16 * (j % 2)
            if name[0] == "f":
                src = win.indirect(T.off[:, lst:lst + 16])
                fin(V.tensor_copy(T.vb[:, c:c + 256], src) if q is V else A.activation(T.vb[:, c:c + 256], src, COPY), k)
            elif name[0] == "d":
                wait(V, K("drawf%d" % j))
                fin(V.tensor_tensor(T.dd[:, c:c + 256], win.indirect(T.off[:, lst + 32:lst + 48]),
                                    T.vb[:, c:c + 256], SUB), k)
            else:
                wait(A, K("drawd%d" % j))
                fin(A.activation(zout[2 * (j % 2) + j // 2], T.dd[:, c:c + 256], ABS), k)
            return
        who, i = "MO".index(name[0]), int(name[1])
        m = 512 >> i
        if i == 1:
            k = K("draw" + name, 2)
            wait(V, K("drawa%d" % (2 * who)), K("drawa%d" % (2 * who + 1)))
            for a, out in ((0, pl), (128, T.l1)):
                fin(V.tensor_tensor(out[:, 128 * who:128 * who + 128] if a else T.pt[:, 256 + 128 * who:384 + 128 * who],
                                    (T.pz0, T.pz1)[who][:, a:a + 128], T.zs[:, 256 * who + a:256 * who + a + 128], ADD), k)
        elif i == 2:
            wait(V, K("draw%s1" % name[0], 2))
            fin(V.tensor_tensor(T.l2[:, m * who:m * who + m], T.pt[:, 256 + m * who:256 + m * who + m],
                                T.l1[:, m * who:m * who + m], ADD), k)
        else:
            src, out = {3: (T.l2, T.l3), 4: (T.l3, T.l4), 5: (T.l4, T.res)}[i]
            c = 2 * m * who
            wait(V, K("draw%s%d" % (name[0], i - 1)))
            if name in TWO:
                out = T.l4m if who == 0 else T.res
                wait(V, k_fill)
                for h in range(2):
                    fin(V.tensor_tensor(out[lo, m * h:m * h + m], src[half[h], c:c + m],
                                        src[half[h], c + m:c + 2 * m], ADD), k)
                return
            fin(V.tensor_tensor(out[:, m * who:m * who + m], src[:, c:c + m], src[:, c + m:c + 2 * m], ADD), k)

    for q, names in ((V, DRAW_V), (A, DRAW_A)):
        for name in names.split():
            (draw if MERGED else draw2)(q, name)

    er = common(rank, [mate])
    if not MERGED:
        named["draw5"] = K("drawO5")
        wait(g, K("drawM4"))
        tr = RemoteDMATransfer(dst_ids=[dst(mate)], dma_engine_mask=_bits(er), remote_sem=T.sem.res,
                               srcs=[T.l4[:, 0:16], T.l4[:, 16:32]], dsts=[T.land[:]], alu_op=1)
        if "M4" in TWO:
            tr = RemoteDMATransfer(dst_ids=[dst(mate)], dma_engine_mask=_bits(er), remote_sem=T.sem.res,
                                   srcs=[T.l4m[:, 0:48], T.l4m[:, 16:64]], dsts=[T.land3[:]], alu_op=1)
    elif FOLD:
        wait(g, K("draw4"))
        tr = RemoteDMATransfer(dst_ids=[dst(mate)], dma_engine_mask=_bits(er), remote_sem=T.sem.res,
                               srcs=[T.l4[:, 0:16], T.l4[:, 32:48]], dsts=[T.land[:]], alu_op=1)
    else:
        wait(g, K("draw5"))
        tr = RemoteDMATransfer(dst_ids=[dst(mate)], dma_engine_mask=_bits(er), remote_sem=T.sem.res,
                               src=T.res[:, 0:16], dst=T.land[:])
    g.remote_dma_fused([tr], local_sem=T.sem.sent)
    sent[1] += len(er)
    k_land = [T.sem.res, len(common(mate, [rank])), "res"]
    stores = {SY_: [] for SY_ in range(2)}
    if "O5" in TWO:
        stores[1].append((K("draw5"), T.y[mine, :], T.res[lo, :]))
    else:
        for h in range(2):
            stores[h].append((K("draw5"), T.y[mine, 16 * h:16 * h + 16], T.res[half[h], 16:32]))
    if "M4" in TWO:
        stores[0].append((k_land, T.y[theirs, :], T.land3[lo, 0:3:2, :]))
    else:
        for h in range(2):
            stores[0 if "O5" in TWO else h].append((k_land, T.y[theirs, 16 * h:16 * h + 16], T.land[half[h], :]))
    for h, q in enumerate((SY, A)):
        k = tok()
        for kk, o, i in stores[h]:
            wait(q, kk)
            mark(q.dma_start(o, i), k, 16)
        wait(q, k)
    wait(g, sent)
